import numpy as np
import ml_dtypes


def mxq(x, axis, fmt="e4m3"):
    dtype, down = {"e4m3": (ml_dtypes.float8_e4m3fn, 7), "e5m2": (ml_dtypes.float8_e5m2, 14)}[fmt]
    v = np.moveaxis(np.asarray(x, np.float32).astype(ml_dtypes.bfloat16).astype(np.float64), axis, -1)
    blocks = v.reshape(v.shape[:-1] + (-1, 32))
    amax = np.abs(blocks).max(-1, keepdims=True)
    byte = np.maximum(np.where(amax > 0, np.frexp(amax)[1] - 1 + 127, 0) - down, 1)
    scale = np.exp2(byte - 127.0)
    codes = (blocks / scale).astype(np.float32).astype(dtype).astype(np.float64)
    return np.moveaxis((codes * scale).reshape(v.shape), -1, axis)


WIDE = False


def mx_kscale(k):
    if not WIDE:
        return np.ones(k)
    levels = np.array([10, -10, 5, -5, 0])
    if k % 512:
        return np.exp2(np.random.permutation(np.resize(levels, k // 32))).repeat(32)
    a = np.empty((k // 512, 16))
    for p in range(k // 512):
        a[p, :8] = np.random.permutation(np.resize(levels, 8))
        for g in range(8):
            far = levels[np.abs(levels - a[p, g]) >= 10]
            a[p, g + 8] = far[np.random.randint(len(far))]
    return np.exp2(a.ravel()).repeat(32)


BF16 = ml_dtypes.bfloat16


def bf(x):
    return np.asarray(x, np.float32).astype(BF16)


def f64(x):
    return np.asarray(x).astype(np.float64)


E2M1 = np.array([0.0, 0.5, 1.0, 1.5, 2.0, 3.0, 4.0, 6.0, -0.0, -0.5, -1.0, -1.5, -2.0, -3.0, -4.0, -6.0])


def pack_weight(w, fmt):
    k, n = w.shape
    w = f64(bf(w)).reshape(k // 32, 32, n)
    amax = np.abs(w).max(1)
    if fmt == "e4m3":
        byte = np.frexp(amax)[1] - 1 + 127 - 7
    else:
        mant, ex = np.frexp(amax / 6.0)
        byte = np.where(mant > 0.5, ex, ex - 1) + 127
    byte = np.clip(np.where(amax > 0, byte, 1), 1, 254)
    scaled = (w * np.exp2(127.0 - byte)[:, None, :]).reshape(k, n).astype(np.float32)
    by_word = np.ascontiguousarray(scaled.reshape(k // 512, 128, 4, n).transpose(0, 1, 3, 2))
    if fmt == "e4m3":
        words = by_word.astype(ml_dtypes.float8_e4m3fn).view(np.uint8)
    else:
        c = by_word.astype(ml_dtypes.float4_e2m1fn).view(np.uint8) & 0xF
        words = c[..., 0::2] | (c[..., 1::2] << 4)
    return np.ascontiguousarray(words), np.ascontiguousarray(byte.astype(np.uint8).reshape(k // 512, 16, n))


def unpack_weight(words, scales, fmt):
    g, p, n, _ = words.shape
    if fmt == "e4m3":
        vals = np.ascontiguousarray(words).view(ml_dtypes.float8_e4m3fn).astype(np.float64)
    else:
        nib = np.empty((g, p, n, 4), np.uint8)
        nib[..., 0::2] = words & 0xF
        nib[..., 1::2] = words >> 4
        vals = E2M1[nib]
    vals = vals * np.repeat(np.exp2(scales.astype(np.float64) - 127.0), 8, axis=1)[..., None]
    return vals.transpose(0, 1, 3, 2).reshape(g * 512, n)
def pack4(w):
    words, scales = pack_weight(w, "e2m1")
    return words.reshape(words.shape[0], 128, -1), scales


def unpack4(words, scales):
    return unpack_weight(words.reshape(words.shape[0], 128, -1, 2), scales, "e2m1")


G, V, M, N, C = 4, 512, 1024, 1024, 512


def draw0():
    s = mx_kscale(G * M)
    t = mx_kscale(N)
    duals = np.random.standard_normal((G, V, M)) * s.reshape(G, 1, M)
    tech = np.random.standard_normal((G * M, N)) / np.sqrt(M) / s[:, None] * t
    tech_words, tech_scales = pack4(tech)
    return {"duals": bf(duals),
            "tech_words": tech_words,
            "tech_scales": tech_scales,
            "cost": bf(0.5 * np.random.standard_normal(N) * t),
            "plans": bf(np.random.standard_normal((C, N)) / np.sqrt(N) / t),
            "intercept": bf(0.5 * np.random.standard_normal((G, V))),
            "estimate": bf(0.5 * np.random.standard_normal((G, C)))}


def core(duals, tech_words, tech_scales, cost, plans, intercept, estimate):
    tech = unpack4(tech_words, tech_scales).reshape(G, M, N)
    dq = mxq(f64(duals), 2, "e4m3")
    pt = dq @ tech
    slope = f64(cost) - pt
    sq = mxq(slope, 2, "e4m3")
    xq = mxq(f64(plans), 1, "e4m3")
    value = sq @ xq.T
    cut = value + f64(intercept)[:, :, None]
    return cut - f64(estimate)[:, None, :]


def e4m3fn_bytes(y):
    return np.clip(np.asarray(y, np.float64), -448.0, 448.0).astype(np.float32).astype(ml_dtypes.float8_e4m3fn).view(np.uint8)


def e4m3fn_values(b):
    return np.asarray(b, np.uint8).view(ml_dtypes.float8_e4m3fn).astype(np.float64)


def setup_inputs():
    d = draw0()
    x0 = np.asarray(d['plans']).astype(np.float64)
    s = (np.max(np.abs(x0), axis=(0,), keepdims=True) / 448.0).astype(np.float32)
    out = {}
    for k, v in d.items():
        if k == 'plans':
            out['plans_bytes'] = e4m3fn_bytes(x0 / s.astype(np.float64))
            out['plans_scale'] = s
        else:
            out[k] = v
    return out


def reference(duals, tech_words, tech_scales, cost, plans_bytes, plans_scale, intercept, estimate):
    return core(duals, tech_words, tech_scales, cost, e4m3fn_values(plans_bytes) * plans_scale.astype(np.float64), intercept, estimate)

@@ -1,0 +1,518 @@
+from contextlib import ExitStack
+
+import concourse.mybir as mybir
+from concourse.masks import make_identity
+
+G, V, M, N, C = 4, 512, 1024, 1024, 512
+FLOPS = G * (2 * V * M * N + 2 * V * N * C)
+
+F32 = mybir.dt.float32
+BF16 = mybir.dt.bfloat16
+I32 = mybir.dt.int32
+U32 = mybir.dt.uint32
+U8 = mybir.dt.uint8
+FP8 = mybir.dt.float8_e4m3fn
+FP8X4 = mybir.dt.float8_e4m3fn_x4
+FP4X4 = mybir.dt.float4_e2m1fn_x4
+ADD = mybir.AluOpType.add
+SUB = mybir.AluOpType.subtract
+MULT = mybir.AluOpType.mult
+IDENTITY = mybir.ActivationFunctionType.Identity
+
+P = 128
+KG = 2
+NH = 2
+NT = 4
+VT = V // P
+CT = C // P
+HALF = 512
+S_SHARE = 128
+
+
+def tile_benders_cut_evaluation_s14_kernel(
+    tc, duals, tech_words, tech_scales, cost, plans_bytes, plans_scale, intercept, estimate, out
+):
+    nc = tc.nc
+    with ExitStack() as ctx:
+        keep = ctx.enter_context(tc.tile_pool(name="keep", bufs=1))
+        work = ctx.enter_context(tc.tile_pool(name="work", bufs=2))
+        outs = ctx.enter_context(tc.tile_pool(name="outs", bufs=6))
+        psum = ctx.enter_context(tc.psum_pool(name="psum", bufs=8))
+        ctx.enter_context(tc.manual_schedule())
+
+        def bank(shape, dtype):
+            return psum.tile(shape, dtype, name="bank", tag="bank")
+
+        ident = keep.tile([P, P], F32, name="ident")
+        ident_bf = keep.tile([P, P], BF16, name="ident_bf")
+        rows = keep.tile([P, P], BF16, name="rows")
+        cols = keep.tile([P, 24], F32, name="cols")
+        warm = keep.tile([P, 8], F32, name="warm")
+        x_raw = [keep.tile([P, VT, M], BF16, name=f"x_raw{z}", align_bytes=64) for z in range(G)]
+        t_raw = [keep.tile([P, KG, 2 * N], U8, name=f"t_raw{z}", align_bytes=64) for z in range(G)]
+        t_words = [keep.tile([P, KG, 2 * N], U8, name=f"t_words{z}", align_bytes=64) for z in range(G)]
+        ts_raw = keep.tile([P, G * KG, N], U8, name="ts_raw", align_bytes=64)
+        ts = keep.tile([P, G * KG, N], U8, name="ts", align_bytes=64)
+        plan_b = keep.tile([P, CT, N], U8, name="plan_b", align_bytes=64)
+        plan_s = keep.tile([P, N], F32, name="plan_s", align_bytes=64)
+        plan_w = keep.tile([P, CT, N], BF16, name="plan_w", align_bytes=64)
+        plan_o = keep.tile([P, CT, N], BF16, name="plan_o", align_bytes=64)
+        plan_g = [keep.tile([P, C, NT], BF16, name=f"plan_g{h}", align_bytes=64) for h in range(NH)]
+        plan_c = [keep.tile([P, C], U32, name=f"plan_c{h}", align_bytes=64) for h in range(NH)]
+        plan_sc = [keep.tile([P, C], U8, name=f"plan_sc{h}", align_bytes=64) for h in range(NH)]
+        est = keep.tile([P, G, C], BF16, name="est", align_bytes=64)
+
+        x_word, x_group, x_code, x_scale, xt = {}, {}, {}, {}, {}
+        s_plane, s_group, s_code, s_scale = {}, {}, {}, {}
+        acc1, acc2, pt = {}, {}, {}
+        copy_v, copy_s = nc.vector.tensor_copy, nc.scalar.copy
+
+        def load_duals(z, u0, u1):
+            nc.sync.dma_start(
+                out=x_raw[z][:, u0:u1, :], in_=duals[z].rearrange("(u p) m -> p u m", p=P)[:, u0:u1, :]
+            )
+
+        def load_tech(z, h0, h1):
+            b = slice(h0 * 2 * HALF, h1 * 2 * HALF)
+            nc.sync.dma_start(
+                out=t_raw[z][:, :, b].bitcast(I32),
+                in_=tech_words[KG * z : KG * (z + 1), :, b].rearrange("g p b -> p g b").bitcast(I32),
+            )
+
+        def load_scales(q, g0, g1):
+            nc.sync.dma_start(
+                out=ts_raw[32 * q : 32 * q + 4, g0:g1, :].bitcast(I32),
+                in_=tech_scales[g0:g1, 4 * q : 4 * q + 4, :].rearrange("g r n -> r g n").bitcast(I32),
+            )
+
+        def load_cost(h):
+            nc.scalar.dma_start(
+                out=rows[NT * h : NT * (h + 1), :].rearrange("t (a q) -> t a q", q=8),
+                in_=cost[h * HALF : (h + 1) * HALF].rearrange("(a t q) -> t a q", t=NT, q=8),
+            )
+
+        def load_intercept():
+            nc.scalar.dma_start(
+                out=rows[NT * NH : NT * NH + G * VT, :], in_=intercept.rearrange("z (u p) -> (z u) p", p=P)
+            )
+
+        def load_plans():
+            nc.sync.dma_start(out=plan_b[:], in_=plans_bytes.rearrange("(c p) n -> p c n", p=P))
+
+        def load_plan_scale():
+            nc.sync.dma_start(out=plan_s[:], in_=plans_scale.rearrange("o n -> (o n)").partition_broadcast(P))
+
+        def load_estimate():
+            nc.sync.dma_start(out=est[:], in_=estimate.partition_broadcast(P))
+
+        def split_words(engine_copy, z, u0, u1):
+            if z not in x_word:
+                x_word[z] = work.tile([P, VT, M], BF16, name="x_word", align_bytes=64)
+            engine_copy(
+                out=x_word[z][:, u0:u1, :].bitcast(F32).rearrange("p u (g e w) -> p (u g) e w", g=KG, e=2),
+                in_=x_raw[z][:, u0:u1, :].bitcast(F32).rearrange("p u (g w e) -> p (u g) e w", g=KG, e=2),
+            )
+
+        def TR(z, u):
+            xt[z, u] = bank([P, KG, 2, P], F32)
+            words = (x_word[z] if z in x_word else x_raw[z])[:, u, :].bitcast(F32)
+            for g in range(KG):
+                for e in range(2):
+                    w = (
+                        words[:, 256 * g + P * e : 256 * g + P * (e + 1)]
+                        if z in x_word
+                        else words[:, 256 * g + e : 256 * (g + 1) : 2]
+                    )
+                    nc.tensor.transpose(xt[z, u][:, g, e, :], w, ident[:])
+
+        def XC(engine_copy, z, u):
+            if z not in x_group:
+                x_group[z] = work.tile([P, KG, V * 4], BF16, name="x_group", align_bytes=64)
+            dst = x_group[z][:].bitcast(F32).rearrange("p g (v e) -> p g v e", e=2)
+            engine_copy(out=dst[:, :, u * P : (u + 1) * P, :], in_=xt[z, u][:].rearrange("p g e r -> p g r e"))
+
+        def DQ(z, g, v0, v1):
+            if z not in x_code:
+                x_code[z] = work.tile([P, KG, V], U32, name="x_code", align_bytes=64)
+                x_scale[z] = work.tile([P, KG, V], U8, name="x_scale", align_bytes=64)
+            nc.vector.quantize_mx(
+                out=x_code[z][:, g, v0:v1].bitcast(FP8X4),
+                scales=x_scale[z][:, g, v0:v1],
+                in_=x_group[z][:, g, 4 * v0 : 4 * v1],
+            )
+
+        def TP(z, h0, h1):
+            w = slice(h0 * HALF // 2, h1 * HALF // 2)
+            for g in range(KG):
+                nc.vector.tensor_copy(
+                    out=t_words[z][:, g, :].bitcast(I32)[:, w].rearrange("p (h t a w) -> p h t a w", t=NT, a=16, w=4),
+                    in_=t_raw[z][:, g, :].bitcast(I32)[:, w].rearrange("p (h a t w) -> p h t a w", t=NT, a=16, w=4),
+                )
+
+        def SP(g0, g1):
+            nc.vector.tensor_copy(
+                out=ts[:, g0:g1, :].bitcast(I32).rearrange("p g (h t a w) -> p (g h) t a w", h=NH, t=NT, w=2),
+                in_=ts_raw[:, g0:g1, :].bitcast(I32).rearrange("p g (h a t w) -> p (g h) t a w", h=NH, t=NT, w=2),
+            )
+
+        def S1(z, h, t):
+            acc1[z, h, t] = bank([P, V], F32)
+            c0 = h * HALF + t * P
+            for g in range(KG):
+                nc.tensor.matmul_mx(
+                    out=acc1[z, h, t][:],
+                    lhsT=t_words[z][:, g, 2 * c0 : 2 * (c0 + P)].bitcast(FP4X4),
+                    lhsT_scale=ts[:, KG * z + g, c0 : c0 + P],
+                    rhs=x_code[z][:, g, :].bitcast(FP8X4),
+                    rhs_scale=x_scale[z][:, g, :],
+                    start=(g == 0),
+                    stop=(g == KG - 1),
+                )
+
+        def EV(z, h, t):
+            if (z, h) not in s_plane:
+                s_plane[z, h] = work.tile([P, NT, V], BF16, name="s_plane", align_bytes=64, bufs=4)
+            j = NT * h + t
+            nc.scalar.activation(
+                out=s_plane[z, h][:, t, :], in_=acc1[z, h, t][:], func=IDENTITY, bias=cols[:, j : j + 1], scale=-1.0
+            )
+
+        def GR(engine_copy, z, h, v0, v1):
+            if (z, h) not in s_group:
+                s_group[z, h] = work.tile([P, V, NT], BF16, name="s_group", align_bytes=64, bufs=4)
+            engine_copy(
+                out=s_group[z, h][:, v0:v1, :].rearrange("p (c i) t -> p c t i", i=4),
+                in_=s_plane[z, h][:, :, v0:v1].rearrange("p t (c i) -> p c t i", i=4),
+            )
+
+        def SQ(z, h, v0, v1):
+            if (z, h) not in s_code:
+                s_code[z, h] = work.tile([P, V], U32, name="s_code", align_bytes=64, bufs=6)
+                s_scale[z, h] = work.tile([P, V], U8, name="s_scale", align_bytes=64, bufs=6)
+            nc.vector.quantize_mx(
+                out=s_code[z, h][:, v0:v1].bitcast(FP8X4),
+                scales=s_scale[z, h][:, v0:v1],
+                in_=s_group[z, h][:, v0:v1, :].rearrange("p v t -> p (v t)"),
+            )
+
+        def S2(z, u, h):
+            if h == 0:
+                acc2[z, u] = bank([P, C], F32)
+            v = slice(u * P, (u + 1) * P)
+            nc.tensor.matmul_mx(
+                out=acc2[z, u][:],
+                lhsT=s_code[z, h][:, v].bitcast(FP8X4),
+                lhsT_scale=s_scale[z, h][:, v],
+                rhs=plan_c[h][:].bitcast(FP8X4),
+                rhs_scale=plan_sc[h][:],
+                start=(h == 0),
+                stop=(h == NH - 1),
+            )
+
+        def FIN(z, u, pieces=1):
+            j = NT * NH + VT * z + u
+            o = outs.tile([P, C], F32, name="o", align_bytes=64)
+            w = C // pieces
+            for c in range(0, C, w):
+                nc.vector.scalar_tensor_tensor(
+                    out=o[:, c : c + w],
+                    in0=acc2[z, u][:, c : c + w],
+                    scalar=cols[:, j : j + 1],
+                    in1=est[:, z, c : c + w],
+                    op0=ADD,
+                    op1=SUB,
+                )
+                nc.sync.dma_start(out=out[z, u * P : (u + 1) * P, c : c + w], in_=o[:, c : c + w])
+
+        def PM(c):
+            nc.vector.tensor_tensor(
+                out=plan_w[:, c, :], in0=plan_b[:, c, :].bitcast(FP8), in1=plan_s[:], op=MULT
+            )
+
+        def PP(engine_copy, c):
+            for h in range(NH):
+                n = slice(h * HALF, (h + 1) * HALF)
+                engine_copy(
+                    out=plan_o[:, c, n].rearrange("p (t a q) -> p t a q", t=NT, q=8),
+                    in_=plan_w[:, c, n].rearrange("p (a t q) -> p t a q", t=NT, q=8),
+                )
+
+        def PT(c, h):
+            pt[c, h] = bank([P, NT, P], BF16)
+            for t in range(NT):
+                n0 = h * HALF + t * P
+                nc.tensor.transpose(pt[c, h][:, t, :], plan_o[:, c, n0 : n0 + P], ident_bf[:])
+
+        def PX(c, h):
+            nc.scalar.copy(out=plan_g[h][:, c * P : (c + 1) * P, :], in_=pt[c, h][:].rearrange("p t c -> p c t"))
+
+        def PQ(h):
+            nc.vector.quantize_mx(
+                out=plan_c[h][:].bitcast(FP8X4),
+                scales=plan_sc[h][:],
+                in_=plan_g[h][:].rearrange("p c t -> p (c t)"),
+            )
+
+        def CTR():
+            acc2["cols"] = bank([P, P], BF16)
+            nc.tensor.transpose(acc2["cols"][:], rows[:], ident_bf[:])
+            nc.vector.tensor_copy(out=cols[:], in_=acc2["cols"][:, 0:24])
+
+        make_identity(nc, ident[:])
+        nc.vector.memset(ts_raw[:, 0:KG, :].bitcast(I32), 0)
+        nc.vector.memset(rows[:], 0.0)
+        nc.vector.memset(warm[:], 0.0)
+        nc.gpsimd.memset(ts_raw[:, KG:, :].bitcast(I32), 0)
+        nc.vector.tensor_copy(out=ident_bf[:], in_=ident[:])
+        nc.scalar.activation(out=warm[:, 4:8], in_=warm[:, 0:4], func=IDENTITY, bias=0.0, scale=1.0)
+
+        load_duals(0, 0, 1)
+        TR(0, 0)
+        load_scales(0, 0, KG)
+        load_duals(0, 1, 2)
+        load_duals(0, 2, 3)
+        load_duals(0, 3, 4)
+        TR(0, 1)
+        load_cost(0)
+        load_tech(0, 0, 1)
+        load_cost(1)
+        XC(copy_s, 0, 0)
+        TR(0, 3)
+        load_scales(1, 0, KG)
+        load_scales(3, 0, KG)
+        TR(0, 2)
+        load_scales(2, 0, KG)
+        load_duals(1, 0, 2)
+        XC(copy_s, 0, 1)
+        load_scales(2, KG, G * KG)
+        load_tech(0, 1, 2)
+        load_intercept()
+        XC(copy_s, 0, 3)
+        load_plans()
+        load_scales(3, KG, G * KG)
+        SP(0, KG)
+        DQ(0, 0, 0, 256)
+        load_scales(1, KG, G * KG)
+        TP(0, 0, 1)
+        DQ(0, 1, 0, 256)
+        XC(copy_s, 0, 2)
+        load_scales(0, KG, G * KG)
+        load_plan_scale()
+        DQ(0, 0, 256, 512)
+        TR(1, 0)
+        DQ(0, 1, 256, 512)
+        TR(1, 1)
+        XC(copy_s, 1, 0)
+        XC(copy_s, 1, 1)
+        CTR()
+        SP(KG, 2 * KG)
+        S1(0, 0, 0)
+        TP(0, 1, 2)
+        DQ(1, 0, 0, 256)
+        PM(2)
+        PM(1)
+        S1(0, 0, 1)
+        S1(0, 0, 3)
+        load_duals(1, 2, 4)
+        EV(0, 0, 0)
+        PM(0)
+        S1(0, 1, 0)
+        S1(0, 1, 3)
+        EV(0, 0, 1)
+        EV(0, 0, 3)
+        S1(0, 1, 1)
+        EV(0, 1, 0)
+        PP(copy_v, 1)
+        PP(copy_v, 0)
+        S1(0, 1, 2)
+        PP(copy_v, 2)
+        EV(0, 1, 1)
+        EV(0, 1, 2)
+        S1(0, 0, 2)
+        TR(1, 2)
+        load_duals(2, 0, 4)
+        TR(1, 3)
+        PT(0, 0)
+        EV(0, 1, 3)
+        PT(1, 0)
+        DQ(1, 1, 0, 256)
+        TR(2, 0)
+        PT(2, 1)
+        SP(2 * KG, 3 * KG)
+        load_tech(1, 0, 2)
+        XC(copy_s, 1, 2)
+        TP(1, 1, 2)
+        EV(0, 0, 2)
+        PT(1, 1)
+        TP(1, 0, 1)
+        XC(copy_s, 1, 3)
+        PT(2, 0)
+        DQ(1, 0, 256, 512)
+        load_estimate()
+        PX(0, 0)
+        load_duals(3, 0, 4)
+        DQ(1, 1, 256, 512)
+        PT(0, 1)
+        XC(copy_s, 2, 0)
+        S1(1, 0, 0)
+        PX(2, 0)
+        S1(1, 0, 3)
+        PM(3)
+        GR(copy_v, 0, 1, 0, 384)
+        PX(1, 0)
+        PX(1, 1)
+        PX(2, 1)
+        S1(1, 0, 1)
+        PX(0, 1)
+        PP(copy_v, 3)
+        S1(1, 0, 2)
+        EV(1, 0, 0)
+        load_tech(2, 0, 2)
+        S1(1, 1, 0)
+        PT(3, 1)
+        GR(copy_s, 0, 1, 384, 512)
+        GR(copy_v, 0, 0, 0, 384)
+        PT(3, 0)
+        TR(2, 2)
+        load_tech(3, 0, 2)
+        GR(copy_s, 0, 0, 384, 512)
+        EV(1, 0, 3)
+        TR(2, 1)
+        EV(1, 0, 1)
+        TP(2, 0, 2)
+        PX(3, 1)
+        SQ(0, 0, 0, 512)
+        PX(3, 0)
+        SQ(0, 1, 0, 512)
+        TR(3, 0)
+        EV(1, 0, 2)
+        PQ(1)
+        TR(2, 3)
+        PQ(0)
+        EV(1, 1, 0)
+        GR(copy_v, 1, 0, 0, 384)
+        XC(copy_s, 2, 1)
+        S1(1, 1, 2)
+        S1(1, 1, 1)
+        S2(0, 3, 0)
+        XC(copy_s, 2, 2)
+        S2(0, 1, 0)
+        XC(copy_s, 2, 3)
+        DQ(2, 0, 0, 256)
+        XC(copy_s, 3, 0)
+        DQ(2, 1, 256, 512)
+        EV(1, 1, 2)
+        GR(copy_s, 1, 0, 384, 512)
+        DQ(2, 1, 0, 256)
+        S1(1, 1, 3)
+        EV(1, 1, 3)
+        S2(0, 1, 1)
+        S2(0, 2, 0)
+        S2(0, 0, 0)
+        S2(0, 0, 1)
+        S2(0, 2, 1)
+        S2(0, 3, 1)
+        DQ(2, 0, 256, 512)
+        EV(1, 1, 1)
+        S1(2, 0, 3)
+        FIN(0, 1)
+        SP(3 * KG, 4 * KG)
+        FIN(0, 3)
+        S1(2, 0, 0)
+        S1(2, 0, 2)
+        S1(2, 1, 0)
+        EV(2, 0, 0)
+        GR(copy_v, 1, 1, 0, 384)
+        GR(copy_s, 1, 1, 384, 512)
+        S1(2, 0, 1)
+        FIN(0, 0)
+        EV(2, 0, 2)
+        FIN(0, 2)
+        TP(3, 0, 2)
+        TR(3, 2)
+        EV(2, 0, 3)
+        EV(2, 0, 1)
+        SQ(1, 0, 0, 512)
+        XC(copy_s, 3, 2)
+        EV(2, 1, 0)
+        TR(3, 3)
+        TR(3, 1)
+        S1(2, 1, 1)
+        SQ(1, 1, 0, 512)
+        S2(1, 0, 0)
+        S1(2, 1, 3)
+        XC(copy_s, 3, 1)
+        GR(copy_v, 2, 0, 0, 384)
+        XC(copy_s, 3, 3)
+        DQ(3, 0, 0, 256)
+        S2(1, 1, 0)
+        EV(2, 1, 1)
+        DQ(3, 1, 0, 256)
+        S1(2, 1, 2)
+        S2(1, 3, 0)
+        DQ(3, 1, 256, 512)
+        GR(copy_s, 2, 0, 384, 512)
+        DQ(3, 0, 256, 512)
+        S2(1, 1, 1)
+        SQ(2, 0, 0, 512)
+        EV(2, 1, 3)
+        S2(1, 0, 1)
+        S1(3, 0, 0)
+        EV(2, 1, 2)
+        FIN(1, 0)
+        S1(3, 0, 2)
+        GR(copy_v, 2, 1, 0, 384)
+        S1(3, 0, 3)
+        FIN(1, 1)
+        S2(1, 3, 1)
+        GR(copy_s, 2, 1, 384, 512)
+        S2(2, 2, 0)
+        S1(3, 0, 1)
+        S1(3, 1, 0)
+        S1(3, 1, 1)
+        SQ(2, 1, 0, 512)
+        FIN(1, 3)
+        S2(2, 2, 1)
+        EV(3, 0, 0)
+        EV(3, 0, 3)
+        EV(3, 0, 2)
+        EV(3, 0, 1)
+        S1(3, 1, 2)
+        S2(2, 1, 0)
+        GR(copy_v, 3, 0, 0, 384)
+        EV(3, 1, 0)
+        GR(copy_s, 3, 0, 384, 512)
+        S1(3, 1, 3)
+        S2(2, 1, 1)
+        S2(2, 0, 0)
+        FIN(2, 2)
+        EV(3, 1, 1)
+        SQ(3, 0, 0, 512)
+        EV(3, 1, 2)
+        S2(2, 3, 0)
+        S2(1, 2, 0)
+        S2(2, 3, 1)
+        S2(2, 0, 1)
+        EV(3, 1, 3)
+        FIN(2, 1)
+        S2(3, 1, 0)
+        GR(copy_v, 3, 1, 0, 256)
+        GR(copy_v, 3, 1, 448, 512)
+        S2(1, 2, 1)
+        SQ(3, 1, 0, 256)
+        S2(3, 0, 0)
+        FIN(2, 0)
+        GR(copy_s, 3, 1, 256, 448)
+        FIN(2, 3)
+        S2(3, 1, 1)
+        S2(3, 0, 1)
+        FIN(3, 0)
+        SQ(3, 1, 256, 512)
+        S2(3, 3, 0)
+        FIN(1, 2)
+        FIN(3, 1)
+        S2(3, 2, 0)
+        S2(3, 3, 1)
+        S2(3, 2, 1)
+        FIN(3, 2)
+        FIN(3, 3, 2)

@@ -86,13 +86,13 @@ def tile_benders_cut_evaluation_s14_kernel(
             )
 
         def load_cost(h):
-            nc.scalar.dma_start(
+            nc.sync.dma_start(
                 out=rows[NT * h : NT * (h + 1), :].rearrange("t (a q) -> t a q", q=8),
                 in_=cost[h * HALF : (h + 1) * HALF].rearrange("(a t q) -> t a q", t=NT, q=8),
             )
 
         def load_intercept():
-            nc.scalar.dma_start(
+            nc.sync.dma_start(
                 out=rows[NT * NH : NT * NH + G * VT, :], in_=intercept.rearrange("z (u p) -> (z u) p", p=P)
             )
 
@@ -258,7 +258,38 @@ def tile_benders_cut_evaluation_s14_kernel(
             nc.tensor.transpose(acc2["cols"][:], rows[:], ident_bf[:])
             nc.vector.tensor_copy(out=cols[:], in_=acc2["cols"][:, 0:24])
 
+        def load_plan_scale_rows(h):
+            nc.sync.dma_start(
+                out=srow[NT * h : NT * (h + 1), :].rearrange("t (a q) -> t a q", q=8),
+                in_=plans_scale[0, h * HALF : (h + 1) * HALF].rearrange("(a t q) -> t a q", t=NT, q=8),
+            )
+
+        def CTS():
+            acc2["scale"] = bank([P, P], F32)
+            nc.tensor.transpose(acc2["scale"][:], srow[:], ident[:])
+            nc.vector.tensor_copy(out=scol[:], in_=acc2["scale"][:, 0:8])
+
+        def CAST(engine_copy, c):
+            engine_copy(out=plan_w[:, c, :], in_=plan_b[:, c, :].bitcast(FP8))
+
+        def PV(c, h):
+            nc.vector.tensor_tensor(
+                out=plan_g[h][:, c * P : (c + 1) * P, :],
+                in0=pt[c, h][:].rearrange("p t c -> p c t"),
+                in1=scol[:, NT * h : NT * (h + 1)].unsqueeze(1).to_broadcast([P, P, NT]),
+                op=MULT,
+            )
+
+        def D():
+            junk = bank([P, V], F32)
+            nc.tensor.matmul(out=junk[:], lhsT=zeros[:, 0:P], rhs=zeros[:], start=True, stop=True)
+
+        zeros = keep.tile([P, V], BF16, name="zeros", align_bytes=64)
+        srow = keep.tile([P, P], F32, name="srow", align_bytes=64)
+        scol = keep.tile([P, 8], F32, name="scol")
+        nc.vector.memset(zeros[:], 0.0)
         make_identity(nc, ident[:])
+        nc.vector.memset(srow[:], 0.0)
         nc.vector.memset(ts_raw[:, 0:KG, :].bitcast(I32), 0)
         nc.vector.memset(rows[:], 0.0)
         nc.vector.memset(warm[:], 0.0)
@@ -267,252 +298,262 @@ def tile_benders_cut_evaluation_s14_kernel(
         nc.scalar.activation(out=warm[:, 4:8], in_=warm[:, 0:4], func=IDENTITY, bias=0.0, scale=1.0)
 
         load_duals(0, 0, 1)
-        TR(0, 0)
         load_scales(0, 0, KG)
-        load_duals(0, 1, 2)
-        load_duals(0, 2, 3)
-        load_duals(0, 3, 4)
-        TR(0, 1)
-        load_cost(0)
-        load_tech(0, 0, 1)
-        load_cost(1)
-        XC(copy_s, 0, 0)
-        TR(0, 3)
         load_scales(1, 0, KG)
-        load_scales(3, 0, KG)
-        TR(0, 2)
         load_scales(2, 0, KG)
-        load_duals(1, 0, 2)
-        XC(copy_s, 0, 1)
-        load_scales(2, KG, G * KG)
-        load_tech(0, 1, 2)
+        load_scales(3, 0, KG)
+        load_duals(0, 1, 2)
+        load_duals(0, 2, 4)
+        load_tech(0, 0, 1)
+        load_cost(0)
+        load_cost(1)
         load_intercept()
-        XC(copy_s, 0, 3)
+        load_duals(1, 0, 2)
+        load_plan_scale_rows(0)
+        load_plan_scale_rows(1)
+        load_tech(0, 1, 2)
         load_plans()
+        load_duals(1, 2, 4)
+        load_tech(1, 0, 2)
+        load_scales(0, KG, G * KG)
+        load_scales(1, KG, G * KG)
+        load_scales(2, KG, G * KG)
         load_scales(3, KG, G * KG)
+        load_duals(2, 0, 4)
+        load_tech(2, 0, 2)
+        load_duals(3, 0, 4)
+        load_tech(3, 0, 2)
+        load_estimate()
+        D()
+        D()
+        D()
+        D()
+        D()
+        D()
+        TR(0, 0)
+        XC(copy_s, 0, 0)
+        TR(0, 1)
+        XC(copy_s, 0, 1)
+        TP(0, 0, 1)
         SP(0, KG)
         DQ(0, 0, 0, 256)
-        load_scales(1, KG, G * KG)
-        TP(0, 0, 1)
         DQ(0, 1, 0, 256)
+        D()
+        D()
+        TR(0, 2)
         XC(copy_s, 0, 2)
-        load_scales(0, KG, G * KG)
-        load_plan_scale()
-        DQ(0, 0, 256, 512)
-        TR(1, 0)
-        DQ(0, 1, 256, 512)
-        TR(1, 1)
-        XC(copy_s, 1, 0)
-        XC(copy_s, 1, 1)
+        TR(0, 3)
+        XC(copy_s, 0, 3)
         CTR()
-        SP(KG, 2 * KG)
-        S1(0, 0, 0)
+        CTS()
+        DQ(0, 0, 256, 512)
+        DQ(0, 1, 256, 512)
         TP(0, 1, 2)
-        DQ(1, 0, 0, 256)
-        PM(2)
-        PM(1)
-        S1(0, 0, 1)
-        S1(0, 0, 3)
-        load_duals(1, 2, 4)
+        D()
+        D()
+        TR(1, 0)
+        XC(copy_s, 1, 0)
+        TR(1, 1)
+        XC(copy_s, 1, 1)
+        S1(0, 0, 0)
         EV(0, 0, 0)
-        PM(0)
-        S1(0, 1, 0)
-        S1(0, 1, 3)
+        S1(0, 0, 1)
         EV(0, 0, 1)
-        EV(0, 0, 3)
-        S1(0, 1, 1)
-        EV(0, 1, 0)
-        PP(copy_v, 1)
-        PP(copy_v, 0)
-        S1(0, 1, 2)
-        PP(copy_v, 2)
-        EV(0, 1, 1)
-        EV(0, 1, 2)
         S1(0, 0, 2)
-        TR(1, 2)
-        load_duals(2, 0, 4)
-        TR(1, 3)
-        PT(0, 0)
-        EV(0, 1, 3)
-        PT(1, 0)
-        DQ(1, 1, 0, 256)
-        TR(2, 0)
-        PT(2, 1)
-        SP(2 * KG, 3 * KG)
-        load_tech(1, 0, 2)
-        XC(copy_s, 1, 2)
-        TP(1, 1, 2)
         EV(0, 0, 2)
-        PT(1, 1)
-        TP(1, 0, 1)
+        S1(0, 0, 3)
+        EV(0, 0, 3)
+        CAST(copy_v, 0)
+        CAST(copy_v, 1)
+        DQ(1, 0, 0, 256)
+        DQ(1, 1, 0, 256)
+        CAST(copy_v, 2)
+        CAST(copy_v, 3)
+        PP(copy_v, 0)
+        TR(1, 2)
+        XC(copy_s, 1, 2)
+        TR(1, 3)
         XC(copy_s, 1, 3)
-        PT(2, 0)
+        S1(0, 1, 0)
+        EV(0, 1, 0)
+        S1(0, 1, 1)
+        EV(0, 1, 1)
+        S1(0, 1, 2)
+        EV(0, 1, 2)
+        S1(0, 1, 3)
+        EV(0, 1, 3)
+        GR(copy_v, 0, 0, 0, 320)
+        PP(copy_v, 1)
+        SP(1 * KG, 2 * KG)
+        TP(1, 0, 2)
         DQ(1, 0, 256, 512)
-        load_estimate()
-        PX(0, 0)
-        load_duals(3, 0, 4)
         DQ(1, 1, 256, 512)
-        PT(0, 1)
-        XC(copy_s, 2, 0)
-        S1(1, 0, 0)
-        PX(2, 0)
-        S1(1, 0, 3)
-        PM(3)
-        GR(copy_v, 0, 1, 0, 384)
-        PX(1, 0)
-        PX(1, 1)
-        PX(2, 1)
-        S1(1, 0, 1)
-        PX(0, 1)
+        PP(copy_v, 2)
         PP(copy_v, 3)
-        S1(1, 0, 2)
+        GR(copy_s, 0, 0, 320, 512)
+        PT(0, 0)
+        PV(0, 0)
+        PT(0, 1)
+        PV(0, 1)
+        PT(1, 0)
+        PV(1, 0)
+        PT(1, 1)
+        PV(1, 1)
+        S1(1, 0, 0)
         EV(1, 0, 0)
-        load_tech(2, 0, 2)
-        S1(1, 1, 0)
-        PT(3, 1)
-        GR(copy_s, 0, 1, 384, 512)
-        GR(copy_v, 0, 0, 0, 384)
-        PT(3, 0)
-        TR(2, 2)
-        load_tech(3, 0, 2)
-        GR(copy_s, 0, 0, 384, 512)
-        EV(1, 0, 3)
-        TR(2, 1)
+        S1(1, 0, 1)
         EV(1, 0, 1)
-        TP(2, 0, 2)
-        PX(3, 1)
-        SQ(0, 0, 0, 512)
-        PX(3, 0)
-        SQ(0, 1, 0, 512)
-        TR(3, 0)
+        S1(1, 0, 2)
         EV(1, 0, 2)
-        PQ(1)
-        TR(2, 3)
-        PQ(0)
+        S1(1, 0, 3)
+        EV(1, 0, 3)
+        GR(copy_v, 0, 1, 0, 320)
+        SQ(0, 0, 0, 512)
+        PT(2, 0)
+        PV(2, 0)
+        PT(2, 1)
+        PV(2, 1)
+        PT(3, 0)
+        PV(3, 0)
+        PT(3, 1)
+        PV(3, 1)
+        GR(copy_s, 0, 1, 320, 512)
+        S1(1, 1, 0)
         EV(1, 1, 0)
-        GR(copy_v, 1, 0, 0, 384)
-        XC(copy_s, 2, 1)
-        S1(1, 1, 2)
         S1(1, 1, 1)
-        S2(0, 3, 0)
-        XC(copy_s, 2, 2)
-        S2(0, 1, 0)
-        XC(copy_s, 2, 3)
-        DQ(2, 0, 0, 256)
-        XC(copy_s, 3, 0)
-        DQ(2, 1, 256, 512)
+        EV(1, 1, 1)
+        S1(1, 1, 2)
         EV(1, 1, 2)
-        GR(copy_s, 1, 0, 384, 512)
-        DQ(2, 1, 0, 256)
         S1(1, 1, 3)
         EV(1, 1, 3)
-        S2(0, 1, 1)
-        S2(0, 2, 0)
+        PQ(0)
+        PQ(1)
+        SQ(0, 1, 0, 512)
+        TR(2, 0)
+        XC(copy_s, 2, 0)
+        TR(2, 1)
+        XC(copy_s, 2, 1)
+        SP(2 * KG, 3 * KG)
+        TP(2, 0, 2)
+        GR(copy_v, 1, 0, 0, 320)
+        DQ(2, 0, 0, 256)
+        DQ(2, 1, 0, 256)
         S2(0, 0, 0)
         S2(0, 0, 1)
-        S2(0, 2, 1)
-        S2(0, 3, 1)
+        S2(0, 1, 0)
+        S2(0, 1, 1)
+        TR(2, 2)
+        XC(copy_s, 2, 2)
+        TR(2, 3)
+        XC(copy_s, 2, 3)
+        GR(copy_s, 1, 0, 320, 512)
+        GR(copy_v, 1, 1, 0, 320)
         DQ(2, 0, 256, 512)
-        EV(1, 1, 1)
-        S1(2, 0, 3)
-        FIN(0, 1)
-        SP(3 * KG, 4 * KG)
-        FIN(0, 3)
-        S1(2, 0, 0)
-        S1(2, 0, 2)
-        S1(2, 1, 0)
-        EV(2, 0, 0)
-        GR(copy_v, 1, 1, 0, 384)
-        GR(copy_s, 1, 1, 384, 512)
-        S1(2, 0, 1)
+        DQ(2, 1, 256, 512)
+        GR(copy_s, 1, 1, 320, 512)
+        S2(0, 2, 0)
+        S2(0, 2, 1)
+        S2(0, 3, 0)
+        S2(0, 3, 1)
         FIN(0, 0)
-        EV(2, 0, 2)
-        FIN(0, 2)
-        TP(3, 0, 2)
-        TR(3, 2)
-        EV(2, 0, 3)
+        FIN(0, 1)
+        S1(2, 0, 0)
+        EV(2, 0, 0)
+        S1(2, 0, 1)
         EV(2, 0, 1)
+        S1(2, 0, 2)
+        EV(2, 0, 2)
+        S1(2, 0, 3)
+        EV(2, 0, 3)
+        FIN(0, 2)
+        FIN(0, 3)
         SQ(1, 0, 0, 512)
-        XC(copy_s, 3, 2)
-        EV(2, 1, 0)
-        TR(3, 3)
-        TR(3, 1)
-        S1(2, 1, 1)
         SQ(1, 1, 0, 512)
-        S2(1, 0, 0)
-        S1(2, 1, 3)
+        TR(3, 0)
+        XC(copy_s, 3, 0)
+        TR(3, 1)
         XC(copy_s, 3, 1)
-        GR(copy_v, 2, 0, 0, 384)
-        XC(copy_s, 3, 3)
+        SP(3 * KG, 4 * KG)
+        TP(3, 0, 2)
         DQ(3, 0, 0, 256)
-        S2(1, 1, 0)
-        EV(2, 1, 1)
         DQ(3, 1, 0, 256)
+        GR(copy_v, 2, 0, 0, 320)
+        S1(2, 1, 0)
+        EV(2, 1, 0)
+        S1(2, 1, 1)
+        EV(2, 1, 1)
         S1(2, 1, 2)
-        S2(1, 3, 0)
-        DQ(3, 1, 256, 512)
-        GR(copy_s, 2, 0, 384, 512)
-        DQ(3, 0, 256, 512)
-        S2(1, 1, 1)
-        SQ(2, 0, 0, 512)
-        EV(2, 1, 3)
-        S2(1, 0, 1)
-        S1(3, 0, 0)
         EV(2, 1, 2)
-        FIN(1, 0)
-        S1(3, 0, 2)
-        GR(copy_v, 2, 1, 0, 384)
-        S1(3, 0, 3)
-        FIN(1, 1)
-        S2(1, 3, 1)
-        GR(copy_s, 2, 1, 384, 512)
-        S2(2, 2, 0)
-        S1(3, 0, 1)
-        S1(3, 1, 0)
-        S1(3, 1, 1)
-        SQ(2, 1, 0, 512)
-        FIN(1, 3)
-        S2(2, 2, 1)
-        EV(3, 0, 0)
-        EV(3, 0, 3)
-        EV(3, 0, 2)
-        EV(3, 0, 1)
-        S1(3, 1, 2)
-        S2(2, 1, 0)
-        GR(copy_v, 3, 0, 0, 384)
-        EV(3, 1, 0)
-        GR(copy_s, 3, 0, 384, 512)
-        S1(3, 1, 3)
-        S2(2, 1, 1)
-        S2(2, 0, 0)
-        FIN(2, 2)
-        EV(3, 1, 1)
-        SQ(3, 0, 0, 512)
-        EV(3, 1, 2)
-        S2(2, 3, 0)
+        S1(2, 1, 3)
+        EV(2, 1, 3)
+        TR(3, 2)
+        XC(copy_s, 3, 2)
+        TR(3, 3)
+        XC(copy_s, 3, 3)
+        GR(copy_v, 2, 1, 0, 320)
+        DQ(3, 0, 256, 512)
+        DQ(3, 1, 256, 512)
+        GR(copy_s, 2, 0, 320, 512)
+        GR(copy_s, 2, 1, 320, 512)
+        S2(1, 0, 0)
+        S2(1, 0, 1)
+        S2(1, 1, 0)
+        S2(1, 1, 1)
         S2(1, 2, 0)
-        S2(2, 3, 1)
-        S2(2, 0, 1)
-        EV(3, 1, 3)
-        FIN(2, 1)
-        S2(3, 1, 0)
-        GR(copy_v, 3, 1, 0, 256)
-        GR(copy_v, 3, 1, 448, 512)
         S2(1, 2, 1)
-        SQ(3, 1, 0, 256)
-        S2(3, 0, 0)
+        S2(1, 3, 0)
+        S2(1, 3, 1)
+        SQ(2, 0, 0, 512)
+        FIN(1, 0)
+        FIN(1, 1)
+        SQ(2, 1, 0, 512)
+        FIN(1, 2)
+        FIN(1, 3)
+        S1(3, 0, 0)
+        EV(3, 0, 0)
+        S1(3, 0, 1)
+        EV(3, 0, 1)
+        S1(3, 0, 2)
+        EV(3, 0, 2)
+        S1(3, 0, 3)
+        EV(3, 0, 3)
+        GR(copy_v, 3, 0, 0, 320)
+        GR(copy_s, 3, 0, 320, 512)
+        S2(2, 0, 0)
+        S2(2, 0, 1)
+        S2(2, 1, 0)
+        S2(2, 1, 1)
         FIN(2, 0)
+        FIN(2, 1)
+        S1(3, 1, 0)
+        EV(3, 1, 0)
+        S1(3, 1, 1)
+        EV(3, 1, 1)
+        S1(3, 1, 2)
+        EV(3, 1, 2)
+        S1(3, 1, 3)
+        EV(3, 1, 3)
+        SQ(3, 0, 0, 512)
+        S2(2, 2, 0)
+        S2(2, 2, 1)
+        S2(2, 3, 0)
+        S2(2, 3, 1)
+        S2(3, 0, 0)
+        S2(3, 1, 0)
+        S2(3, 2, 0)
+        S2(3, 3, 0)
+        GR(copy_v, 3, 1, 0, 256)
         GR(copy_s, 3, 1, 256, 448)
+        GR(copy_v, 3, 1, 448, 512)
+        SQ(3, 1, 0, 256)
+        SQ(3, 1, 256, 512)
+        FIN(2, 2)
         FIN(2, 3)
-        S2(3, 1, 1)
         S2(3, 0, 1)
         FIN(3, 0)
-        SQ(3, 1, 256, 512)
-        S2(3, 3, 0)
-        FIN(1, 2)
+        S2(3, 1, 1)
         FIN(3, 1)
-        S2(3, 2, 0)
-        S2(3, 3, 1)
         S2(3, 2, 1)
         FIN(3, 2)
+        S2(3, 3, 1)
         FIN(3, 3, 2)

@@ -48,19 +48,19 @@ def tile_benders_cut_evaluation_s14_kernel(
         rows = keep.tile([P, P], BF16, name="rows")
         cols = keep.tile([P, 24], F32, name="cols")
         warm = keep.tile([P, 8], F32, name="warm")
-        x_raw = [keep.tile([P, VT, M], BF16, name=f"x_raw{z}", align_bytes=64) for z in range(G)]
-        t_raw = [keep.tile([P, KG, 2 * N], U8, name=f"t_raw{z}", align_bytes=64) for z in range(G)]
-        t_words = [keep.tile([P, KG, 2 * N], U8, name=f"t_words{z}", align_bytes=64) for z in range(G)]
-        ts_raw = keep.tile([P, G * KG, N], U8, name="ts_raw", align_bytes=64)
-        ts = keep.tile([P, G * KG, N], U8, name="ts", align_bytes=64)
-        plan_b = keep.tile([P, CT, N], U8, name="plan_b", align_bytes=64)
-        plan_s = keep.tile([P, N], F32, name="plan_s", align_bytes=64)
-        plan_w = keep.tile([P, CT, N], BF16, name="plan_w", align_bytes=64)
-        plan_o = keep.tile([P, CT, N], BF16, name="plan_o", align_bytes=64)
-        plan_g = [keep.tile([P, C, NT], BF16, name=f"plan_g{h}", align_bytes=64) for h in range(NH)]
-        plan_c = [keep.tile([P, C], U32, name=f"plan_c{h}", align_bytes=64) for h in range(NH)]
-        plan_sc = [keep.tile([P, C], U8, name=f"plan_sc{h}", align_bytes=64) for h in range(NH)]
-        est = keep.tile([P, G, C], BF16, name="est", align_bytes=64)
+        x_raw = [keep.tile([P, VT, M], BF16, name=f"x_raw{z}", align_bytes=256) for z in range(G)]
+        t_raw = [keep.tile([P, KG, 2 * N], U8, name=f"t_raw{z}", align_bytes=256) for z in range(G)]
+        t_words = [keep.tile([P, KG, 2 * N], U8, name=f"t_words{z}", align_bytes=256) for z in range(G)]
+        ts_raw = keep.tile([P, G * KG, N], U8, name="ts_raw", align_bytes=256)
+        ts = keep.tile([P, G * KG, N], U8, name="ts", align_bytes=256)
+        plan_b = keep.tile([P, CT, N], U8, name="plan_b", align_bytes=256)
+        plan_s = keep.tile([P, N], F32, name="plan_s", align_bytes=256)
+        plan_w = keep.tile([P, CT, N], BF16, name="plan_w", align_bytes=256)
+        plan_o = keep.tile([P, CT, N], BF16, name="plan_o", align_bytes=256)
+        plan_g = keep.tile([P, NH, C, NT], BF16, name="plan_g", align_bytes=256)
+        plan_c = [keep.tile([P, C], U32, name=f"plan_c{h}", align_bytes=256) for h in range(NH)]
+        plan_sc = [keep.tile([P, C], U8, name=f"plan_sc{h}", align_bytes=256) for h in range(NH)]
+        est = keep.tile([P, G, C], BF16, name="est", align_bytes=256)
 
         x_word, x_group, x_code, x_scale, xt = {}, {}, {}, {}, {}
         s_plane, s_group, s_code, s_scale = {}, {}, {}, {}
@@ -107,7 +107,7 @@ def tile_benders_cut_evaluation_s14_kernel(
 
         def split_words(engine_copy, z, u0, u1):
             if z not in x_word:
-                x_word[z] = work.tile([P, VT, M], BF16, name="x_word", align_bytes=64)
+                x_word[z] = work.tile([P, VT, M], BF16, name="x_word", align_bytes=256)
             engine_copy(
                 out=x_word[z][:, u0:u1, :].bitcast(F32).rearrange("p u (g e w) -> p (u g) e w", g=KG, e=2),
                 in_=x_raw[z][:, u0:u1, :].bitcast(F32).rearrange("p u (g w e) -> p (u g) e w", g=KG, e=2),
@@ -127,14 +127,14 @@ def tile_benders_cut_evaluation_s14_kernel(
 
         def XC(engine_copy, z, u):
             if z not in x_group:
-                x_group[z] = work.tile([P, KG, V * 4], BF16, name="x_group", align_bytes=64)
+                x_group[z] = work.tile([P, KG, V * 4], BF16, name="x_group", align_bytes=256)
             dst = x_group[z][:].bitcast(F32).rearrange("p g (v e) -> p g v e", e=2)
             engine_copy(out=dst[:, :, u * P : (u + 1) * P, :], in_=xt[z, u][:].rearrange("p g e r -> p g r e"))
 
         def DQ(z, g, v0, v1):
             if z not in x_code:
-                x_code[z] = work.tile([P, KG, V], U32, name="x_code", align_bytes=64)
-                x_scale[z] = work.tile([P, KG, V], U8, name="x_scale", align_bytes=64)
+                x_code[z] = work.tile([P, KG, V], U32, name="x_code", align_bytes=256)
+                x_scale[z] = work.tile([P, KG, V], U8, name="x_scale", align_bytes=256)
             nc.vector.quantize_mx(
                 out=x_code[z][:, g, v0:v1].bitcast(FP8X4),
                 scales=x_scale[z][:, g, v0:v1],
@@ -143,11 +143,15 @@ def tile_benders_cut_evaluation_s14_kernel(
 
         def TP(z, h0, h1):
             w = slice(h0 * HALF // 2, h1 * HALF // 2)
-            for g in range(KG):
-                nc.vector.tensor_copy(
-                    out=t_words[z][:, g, :].bitcast(I32)[:, w].rearrange("p (h t a w) -> p h t a w", t=NT, a=16, w=4),
-                    in_=t_raw[z][:, g, :].bitcast(I32)[:, w].rearrange("p (h a t w) -> p h t a w", t=NT, a=16, w=4),
-                )
+            dst = t_words[z][:].bitcast(I32)[:, :, w]
+            src = t_raw[z][:].bitcast(I32)[:, :, w]
+            if h1 - h0 == NH:
+                dst = dst.rearrange("p g (h t a w) -> p (g h) t a w", h=NH, t=NT, w=4)
+                src = src.rearrange("p g (h a t w) -> p (g h) t a w", h=NH, t=NT, w=4)
+            else:
+                dst = dst.rearrange("p g (t a w) -> p g t a w", t=NT, w=4)
+                src = src.rearrange("p g (a t w) -> p g t a w", t=NT, w=4)
+            nc.vector.tensor_copy(out=dst, in_=src)
 
         def SP(g0, g1):
             nc.vector.tensor_copy(
@@ -171,7 +175,7 @@ def tile_benders_cut_evaluation_s14_kernel(
 
         def EV(z, h, t):
             if (z, h) not in s_plane:
-                s_plane[z, h] = work.tile([P, NT, V], BF16, name="s_plane", align_bytes=64, bufs=4)
+                s_plane[z, h] = work.tile([P, NT, V], BF16, name="s_plane", align_bytes=256, bufs=4)
             j = NT * h + t
             nc.scalar.activation(
                 out=s_plane[z, h][:, t, :], in_=acc1[z, h, t][:], func=IDENTITY, bias=cols[:, j : j + 1], scale=-1.0
@@ -179,7 +183,7 @@ def tile_benders_cut_evaluation_s14_kernel(
 
         def GR(engine_copy, z, h, v0, v1):
             if (z, h) not in s_group:
-                s_group[z, h] = work.tile([P, V, NT], BF16, name="s_group", align_bytes=64, bufs=4)
+                s_group[z, h] = work.tile([P, V, NT], BF16, name="s_group", align_bytes=256, bufs=4)
             engine_copy(
                 out=s_group[z, h][:, v0:v1, :].rearrange("p (c i) t -> p c t i", i=4),
                 in_=s_plane[z, h][:, :, v0:v1].rearrange("p t (c i) -> p c t i", i=4),
@@ -187,8 +191,8 @@ def tile_benders_cut_evaluation_s14_kernel(
 
         def SQ(z, h, v0, v1):
             if (z, h) not in s_code:
-                s_code[z, h] = work.tile([P, V], U32, name="s_code", align_bytes=64, bufs=6)
-                s_scale[z, h] = work.tile([P, V], U8, name="s_scale", align_bytes=64, bufs=6)
+                s_code[z, h] = work.tile([P, V], U32, name="s_code", align_bytes=256, bufs=6)
+                s_scale[z, h] = work.tile([P, V], U8, name="s_scale", align_bytes=256, bufs=6)
             nc.vector.quantize_mx(
                 out=s_code[z, h][:, v0:v1].bitcast(FP8X4),
                 scales=s_scale[z, h][:, v0:v1],
@@ -211,7 +215,7 @@ def tile_benders_cut_evaluation_s14_kernel(
 
         def FIN(z, u, pieces=1):
             j = NT * NH + VT * z + u
-            o = outs.tile([P, C], F32, name="o", align_bytes=64)
+            o = outs.tile([P, C], F32, name="o", align_bytes=256)
             w = C // pieces
             for c in range(0, C, w):
                 nc.vector.scalar_tensor_tensor(
@@ -237,20 +241,21 @@ def tile_benders_cut_evaluation_s14_kernel(
                     in_=plan_w[:, c, n].rearrange("p (a t q) -> p t a q", t=NT, q=8),
                 )
 
-        def PT(c, h):
-            pt[c, h] = bank([P, NT, P], BF16)
-            for t in range(NT):
-                n0 = h * HALF + t * P
-                nc.tensor.transpose(pt[c, h][:, t, :], plan_o[:, c, n0 : n0 + P], ident_bf[:])
+        def PT(c):
+            pt[c] = bank([P, NH, NT, P], BF16)
+            for h in range(NH):
+                for t in range(NT):
+                    n0 = h * HALF + t * P
+                    nc.tensor.transpose(pt[c][:, h, t, :], plan_o[:, c, n0 : n0 + P], ident_bf[:])
 
-        def PX(c, h):
-            nc.scalar.copy(out=plan_g[h][:, c * P : (c + 1) * P, :], in_=pt[c, h][:].rearrange("p t c -> p c t"))
+        def PX(c):
+            nc.scalar.copy(out=plan_g[:, :, c * P : (c + 1) * P, :], in_=pt[c][:].rearrange("p h t c -> p h c t"))
 
         def PQ(h):
             nc.vector.quantize_mx(
                 out=plan_c[h][:].bitcast(FP8X4),
                 scales=plan_sc[h][:],
-                in_=plan_g[h][:].rearrange("p c t -> p (c t)"),
+                in_=plan_g[:, h, :, :].rearrange("p c t -> p (c t)"),
             )
 
         def CTR():
@@ -269,14 +274,21 @@ def tile_benders_cut_evaluation_s14_kernel(
             nc.tensor.transpose(acc2["scale"][:], srow[:], ident[:])
             nc.vector.tensor_copy(out=scol[:], in_=acc2["scale"][:, 0:8])
 
-        def CAST(engine_copy, c):
-            engine_copy(out=plan_w[:, c, :], in_=plan_b[:, c, :].bitcast(FP8))
+        def CAST(engine_copy, c0, c1):
+            engine_copy(out=plan_w[:, c0:c1, :], in_=plan_b[:, c0:c1, :].bitcast(FP8))
 
-        def PV(c, h):
+        def PT2(i, h):
+            pt[i, h] = bank([P, 2, NT, P], BF16)
+            for b in range(2):
+                for t in range(NT):
+                    n0 = h * HALF + t * P
+                    nc.tensor.transpose(pt[i, h][:, b, t, :], plan_o[:, 2 * i + b, n0 : n0 + P], ident_bf[:])
+
+        def PV2(i, h):
             nc.vector.tensor_tensor(
-                out=plan_g[h][:, c * P : (c + 1) * P, :],
-                in0=pt[c, h][:].rearrange("p t c -> p c t"),
-                in1=scol[:, NT * h : NT * (h + 1)].unsqueeze(1).to_broadcast([P, P, NT]),
+                out=plan_g[:, h, 2 * i * P : 2 * (i + 1) * P, :].rearrange("p (b c) t -> p b c t", b=2),
+                in0=pt[i, h][:].rearrange("p b t c -> p b c t"),
+                in1=scol[:, NT * h : NT * (h + 1)].unsqueeze(1).unsqueeze(1).to_broadcast([P, 2, P, NT]),
                 op=MULT,
             )
 
@@ -284,14 +296,14 @@ def tile_benders_cut_evaluation_s14_kernel(
             junk = bank([P, V], F32)
             nc.tensor.matmul(out=junk[:], lhsT=zeros[:, 0:P], rhs=zeros[:], start=True, stop=True)
 
-        zeros = keep.tile([P, V], BF16, name="zeros", align_bytes=64)
-        srow = keep.tile([P, P], F32, name="srow", align_bytes=64)
+        zeros = keep.tile([P, V], BF16, name="zeros", align_bytes=256)
+        srow = keep.tile([P, P], F32, name="srow", align_bytes=256)
         scol = keep.tile([P, 8], F32, name="scol")
         nc.vector.memset(zeros[:], 0.0)
         make_identity(nc, ident[:])
-        nc.vector.memset(srow[:], 0.0)
         nc.vector.memset(ts_raw[:, 0:KG, :].bitcast(I32), 0)
         nc.vector.memset(rows[:], 0.0)
+        nc.vector.memset(srow[:], 0.0)
         nc.vector.memset(warm[:], 0.0)
         nc.gpsimd.memset(ts_raw[:, KG:, :].bitcast(I32), 0)
         nc.vector.tensor_copy(out=ident_bf[:], in_=ident[:])
@@ -334,10 +346,9 @@ def tile_benders_cut_evaluation_s14_kernel(
         XC(copy_s, 0, 0)
         TR(0, 1)
         XC(copy_s, 0, 1)
-        TP(0, 0, 1)
-        SP(0, KG)
         DQ(0, 0, 0, 256)
         DQ(0, 1, 0, 256)
+        TP(0, 0, 1)
         D()
         D()
         TR(0, 2)
@@ -348,6 +359,7 @@ def tile_benders_cut_evaluation_s14_kernel(
         CTS()
         DQ(0, 0, 256, 512)
         DQ(0, 1, 256, 512)
+        SP(0, KG)
         TP(0, 1, 2)
         D()
         D()
@@ -363,17 +375,16 @@ def tile_benders_cut_evaluation_s14_kernel(
         EV(0, 0, 2)
         S1(0, 0, 3)
         EV(0, 0, 3)
-        CAST(copy_v, 0)
-        CAST(copy_v, 1)
-        DQ(1, 0, 0, 256)
-        DQ(1, 1, 0, 256)
-        CAST(copy_v, 2)
-        CAST(copy_v, 3)
+        CAST(copy_v, 0, 2)
+        CAST(copy_v, 2, 4)
         PP(copy_v, 0)
+        PP(copy_v, 1)
         TR(1, 2)
         XC(copy_s, 1, 2)
         TR(1, 3)
         XC(copy_s, 1, 3)
+        TP(1, 0, 2)
+        SP(KG, G * KG)
         S1(0, 1, 0)
         EV(0, 1, 0)
         S1(0, 1, 1)
@@ -382,23 +393,16 @@ def tile_benders_cut_evaluation_s14_kernel(
         EV(0, 1, 2)
         S1(0, 1, 3)
         EV(0, 1, 3)
-        GR(copy_v, 0, 0, 0, 320)
-        PP(copy_v, 1)
-        SP(1 * KG, 2 * KG)
-        TP(1, 0, 2)
-        DQ(1, 0, 256, 512)
-        DQ(1, 1, 256, 512)
+        DQ(1, 0, 0, 512)
+        DQ(1, 1, 0, 512)
         PP(copy_v, 2)
         PP(copy_v, 3)
+        GR(copy_v, 0, 0, 0, 320)
         GR(copy_s, 0, 0, 320, 512)
-        PT(0, 0)
-        PV(0, 0)
-        PT(0, 1)
-        PV(0, 1)
-        PT(1, 0)
-        PV(1, 0)
-        PT(1, 1)
-        PV(1, 1)
+        PT2(0, 0)
+        PV2(0, 0)
+        PT2(0, 1)
+        PV2(0, 1)
         S1(1, 0, 0)
         EV(1, 0, 0)
         S1(1, 0, 1)
@@ -407,17 +411,13 @@ def tile_benders_cut_evaluation_s14_kernel(
         EV(1, 0, 2)
         S1(1, 0, 3)
         EV(1, 0, 3)
-        GR(copy_v, 0, 1, 0, 320)
+        GR(copy_v, 0, 1, 0, 256)
+        GR(copy_s, 0, 1, 256, 512)
+        PT2(1, 0)
+        PV2(1, 0)
+        PT2(1, 1)
+        PV2(1, 1)
         SQ(0, 0, 0, 512)
-        PT(2, 0)
-        PV(2, 0)
-        PT(2, 1)
-        PV(2, 1)
-        PT(3, 0)
-        PV(3, 0)
-        PT(3, 1)
-        PV(3, 1)
-        GR(copy_s, 0, 1, 320, 512)
         S1(1, 1, 0)
         EV(1, 1, 0)
         S1(1, 1, 1)
@@ -433,11 +433,11 @@ def tile_benders_cut_evaluation_s14_kernel(
         XC(copy_s, 2, 0)
         TR(2, 1)
         XC(copy_s, 2, 1)
-        SP(2 * KG, 3 * KG)
+        GR(copy_s, 1, 0, 256, 512)
         TP(2, 0, 2)
-        GR(copy_v, 1, 0, 0, 320)
         DQ(2, 0, 0, 256)
         DQ(2, 1, 0, 256)
+        GR(copy_v, 1, 0, 0, 256)
         S2(0, 0, 0)
         S2(0, 0, 1)
         S2(0, 1, 0)
@@ -446,17 +446,18 @@ def tile_benders_cut_evaluation_s14_kernel(
         XC(copy_s, 2, 2)
         TR(2, 3)
         XC(copy_s, 2, 3)
-        GR(copy_s, 1, 0, 320, 512)
-        GR(copy_v, 1, 1, 0, 320)
+        GR(copy_s, 1, 1, 192, 512)
+        GR(copy_v, 1, 1, 0, 192)
         DQ(2, 0, 256, 512)
         DQ(2, 1, 256, 512)
-        GR(copy_s, 1, 1, 320, 512)
+        SQ(1, 0, 0, 512)
         S2(0, 2, 0)
         S2(0, 2, 1)
         S2(0, 3, 0)
         S2(0, 3, 1)
         FIN(0, 0)
         FIN(0, 1)
+        FIN(0, 2)
         S1(2, 0, 0)
         EV(2, 0, 0)
         S1(2, 0, 1)
@@ -465,18 +466,14 @@ def tile_benders_cut_evaluation_s14_kernel(
         EV(2, 0, 2)
         S1(2, 0, 3)
         EV(2, 0, 3)
-        FIN(0, 2)
         FIN(0, 3)
-        SQ(1, 0, 0, 512)
         SQ(1, 1, 0, 512)
+        TP(3, 0, 2)
         TR(3, 0)
         XC(copy_s, 3, 0)
         TR(3, 1)
         XC(copy_s, 3, 1)
-        SP(3 * KG, 4 * KG)
-        TP(3, 0, 2)
-        DQ(3, 0, 0, 256)
-        DQ(3, 1, 0, 256)
+        GR(copy_s, 2, 0, 320, 512)
         GR(copy_v, 2, 0, 0, 320)
         S1(2, 1, 0)
         EV(2, 1, 0)
@@ -490,11 +487,11 @@ def tile_benders_cut_evaluation_s14_kernel(
         XC(copy_s, 3, 2)
         TR(3, 3)
         XC(copy_s, 3, 3)
-        GR(copy_v, 2, 1, 0, 320)
-        DQ(3, 0, 256, 512)
-        DQ(3, 1, 256, 512)
-        GR(copy_s, 2, 0, 320, 512)
-        GR(copy_s, 2, 1, 320, 512)
+        SQ(2, 0, 0, 512)
+        GR(copy_v, 2, 1, 0, 192)
+        DQ(3, 0, 0, 512)
+        DQ(3, 1, 0, 512)
+        GR(copy_s, 2, 1, 192, 512)
         S2(1, 0, 0)
         S2(1, 0, 1)
         S2(1, 1, 0)
@@ -503,7 +500,6 @@ def tile_benders_cut_evaluation_s14_kernel(
         S2(1, 2, 1)
         S2(1, 3, 0)
         S2(1, 3, 1)
-        SQ(2, 0, 0, 512)
         FIN(1, 0)
         FIN(1, 1)
         SQ(2, 1, 0, 512)

@@ -233,13 +233,11 @@ def tile_benders_cut_evaluation_s14_kernel(
                 out=plan_w[:, c, :], in0=plan_b[:, c, :].bitcast(FP8), in1=plan_s[:], op=MULT
             )
 
-        def PP(engine_copy, c):
-            for h in range(NH):
-                n = slice(h * HALF, (h + 1) * HALF)
-                engine_copy(
-                    out=plan_o[:, c, n].rearrange("p (t a q) -> p t a q", t=NT, q=8),
-                    in_=plan_w[:, c, n].rearrange("p (a t q) -> p t a q", t=NT, q=8),
-                )
+        def PP(engine_copy, c0, c1):
+            engine_copy(
+                out=plan_o[:, c0:c1, :].rearrange("p c (h t a q) -> p (c h) t a q", h=NH, t=NT, q=8),
+                in_=plan_w[:, c0:c1, :].rearrange("p c (h a t q) -> p (c h) t a q", h=NH, t=NT, q=8),
+            )
 
         def PT(c):
             pt[c] = bank([P, NH, NT, P], BF16)
@@ -299,9 +297,9 @@ def tile_benders_cut_evaluation_s14_kernel(
         zeros = keep.tile([P, V], BF16, name="zeros", align_bytes=256)
         srow = keep.tile([P, P], F32, name="srow", align_bytes=256)
         scol = keep.tile([P, 8], F32, name="scol")
-        nc.vector.memset(zeros[:], 0.0)
         make_identity(nc, ident[:])
         nc.vector.memset(ts_raw[:, 0:KG, :].bitcast(I32), 0)
+        nc.vector.memset(zeros[:], 0.0)
         nc.vector.memset(rows[:], 0.0)
         nc.vector.memset(srow[:], 0.0)
         nc.vector.memset(warm[:], 0.0)
@@ -310,11 +308,11 @@ def tile_benders_cut_evaluation_s14_kernel(
         nc.scalar.activation(out=warm[:, 4:8], in_=warm[:, 0:4], func=IDENTITY, bias=0.0, scale=1.0)
 
         load_duals(0, 0, 1)
+        load_duals(0, 1, 2)
         load_scales(0, 0, KG)
         load_scales(1, 0, KG)
         load_scales(2, 0, KG)
         load_scales(3, 0, KG)
-        load_duals(0, 1, 2)
         load_duals(0, 2, 4)
         load_tech(0, 0, 1)
         load_cost(0)
@@ -377,8 +375,7 @@ def tile_benders_cut_evaluation_s14_kernel(
         EV(0, 0, 3)
         CAST(copy_v, 0, 2)
         CAST(copy_v, 2, 4)
-        PP(copy_v, 0)
-        PP(copy_v, 1)
+        PP(copy_v, 0, 2)
         TR(1, 2)
         XC(copy_s, 1, 2)
         TR(1, 3)
@@ -395,8 +392,7 @@ def tile_benders_cut_evaluation_s14_kernel(
         EV(0, 1, 3)
         DQ(1, 0, 0, 512)
         DQ(1, 1, 0, 512)
-        PP(copy_v, 2)
-        PP(copy_v, 3)
+        PP(copy_v, 2, 4)
         GR(copy_v, 0, 0, 0, 320)
         GR(copy_s, 0, 0, 320, 512)
         PT2(0, 0)
@@ -538,12 +534,12 @@ def tile_benders_cut_evaluation_s14_kernel(
         S2(3, 1, 0)
         S2(3, 2, 0)
         S2(3, 3, 0)
+        FIN(2, 2)
         GR(copy_v, 3, 1, 0, 256)
         GR(copy_s, 3, 1, 256, 448)
         GR(copy_v, 3, 1, 448, 512)
         SQ(3, 1, 0, 256)
         SQ(3, 1, 256, 512)
-        FIN(2, 2)
         FIN(2, 3)
         S2(3, 0, 1)
         FIN(3, 0)

@@ -3,8 +3,8 @@ from contextlib import ExitStack
 import concourse.mybir as mybir
 from concourse.masks import make_identity
 
-G, V, M, N, C = 4, 512, 1024, 1024, 512
-FLOPS = G * (2 * V * M * N + 2 * V * N * C)
+SCENARIOS, CUTS, ROWS, VARS, PLANS = 4, 512, 1024, 1024, 512
+FLOPS = SCENARIOS * (2 * CUTS * ROWS * VARS + 2 * CUTS * VARS * PLANS)
 
 F32 = mybir.dt.float32
 BF16 = mybir.dt.bfloat16
@@ -20,19 +20,26 @@ MULT = mybir.AluOpType.mult
 IDENTITY = mybir.ActivationFunctionType.Identity
 
 P = 128
-KG = 2
-NH = 2
-NT = 4
-VT = V // P
-CT = C // P
-HALF = 512
-S_SHARE = 128
+T = 4
+PASS = P * T
+ROW_PASSES = ROWS // PASS
+VAR_PASSES = VARS // PASS
+RUN = 8
+CUT_TILES = CUTS // P
+PLAN_TILES = PLANS // P
+COST_COL, INTERCEPT_COL = 0, VAR_PASSES * T
+CONST_COLS = INTERCEPT_COL + SCENARIOS * CUT_TILES
+ALIGN = 256
+
+SCALAR_CUTS = (192, 320)
 
 
 def tile_benders_cut_evaluation_s14_kernel(
     tc, duals, tech_words, tech_scales, cost, plans_bytes, plans_scale, intercept, estimate, out
 ):
     nc = tc.nc
+    copy_v, copy_s = nc.vector.tensor_copy, nc.scalar.copy
+
     with ExitStack() as ctx:
         keep = ctx.enter_context(tc.tile_pool(name="keep", bufs=1))
         work = ctx.enter_context(tc.tile_pool(name="work", bufs=2))
@@ -43,509 +50,372 @@ def tile_benders_cut_evaluation_s14_kernel(
         def bank(shape, dtype):
             return psum.tile(shape, dtype, name="bank", tag="bank")
 
+        def by_scenario(name, shape, dtype):
+            return [keep.tile(shape, dtype, name=f"{name}{z}", align_bytes=ALIGN) for z in range(SCENARIOS)]
+
         ident = keep.tile([P, P], F32, name="ident")
         ident_bf = keep.tile([P, P], BF16, name="ident_bf")
-        rows = keep.tile([P, P], BF16, name="rows")
-        cols = keep.tile([P, 24], F32, name="cols")
-        warm = keep.tile([P, 8], F32, name="warm")
-        x_raw = [keep.tile([P, VT, M], BF16, name=f"x_raw{z}", align_bytes=256) for z in range(G)]
-        t_raw = [keep.tile([P, KG, 2 * N], U8, name=f"t_raw{z}", align_bytes=256) for z in range(G)]
-        t_words = [keep.tile([P, KG, 2 * N], U8, name=f"t_words{z}", align_bytes=256) for z in range(G)]
-        ts_raw = keep.tile([P, G * KG, N], U8, name="ts_raw", align_bytes=256)
-        ts = keep.tile([P, G * KG, N], U8, name="ts", align_bytes=256)
-        plan_b = keep.tile([P, CT, N], U8, name="plan_b", align_bytes=256)
-        plan_s = keep.tile([P, N], F32, name="plan_s", align_bytes=256)
-        plan_w = keep.tile([P, CT, N], BF16, name="plan_w", align_bytes=256)
-        plan_o = keep.tile([P, CT, N], BF16, name="plan_o", align_bytes=256)
-        plan_g = keep.tile([P, NH, C, NT], BF16, name="plan_g", align_bytes=256)
-        plan_c = [keep.tile([P, C], U32, name=f"plan_c{h}", align_bytes=256) for h in range(NH)]
-        plan_sc = [keep.tile([P, C], U8, name=f"plan_sc{h}", align_bytes=256) for h in range(NH)]
-        est = keep.tile([P, G, C], BF16, name="est", align_bytes=256)
+        zeros = keep.tile([P, CUTS], BF16, name="zeros", align_bytes=ALIGN)
+        first_act = keep.tile([P, 8], F32, name="first_act")
+        const_rows = keep.tile([P, P], BF16, name="const_rows")
+        const_cols = keep.tile([P, CONST_COLS], F32, name="const_cols")
+        scale_rows = keep.tile([P, P], F32, name="scale_rows", align_bytes=ALIGN)
+        scale_cols = keep.tile([P, VAR_PASSES * T], F32, name="scale_cols")
+        est = keep.tile([P, SCENARIOS, PLANS], BF16, name="est", align_bytes=ALIGN)
 
-        x_word, x_group, x_code, x_scale, xt = {}, {}, {}, {}, {}
+        x_raw = by_scenario("x_raw", [P, CUT_TILES, ROWS], BF16)
+        w_raw = by_scenario("w_raw", [P, ROW_PASSES, 2 * VARS], U8)
+        w_code = by_scenario("w_code", [P, ROW_PASSES, 2 * VARS], U8)
+        w_scale_raw = keep.tile([P, SCENARIOS * ROW_PASSES, VARS], U8, name="w_scale_raw", align_bytes=ALIGN)
+        w_scale = keep.tile([P, SCENARIOS * ROW_PASSES, VARS], U8, name="w_scale", align_bytes=ALIGN)
+
+        plan_bytes = keep.tile([P, PLAN_TILES, VARS], U8, name="plan_bytes", align_bytes=ALIGN)
+        plan_wide = keep.tile([P, PLAN_TILES, VARS], BF16, name="plan_wide", align_bytes=ALIGN)
+        plan_order = keep.tile([P, PLAN_TILES, VARS], BF16, name="plan_order", align_bytes=ALIGN)
+        plan_group = keep.tile([P, VAR_PASSES, PLANS, T], BF16, name="plan_group", align_bytes=ALIGN)
+        plan_code = keep.tile([P, VAR_PASSES, PLANS], U32, name="plan_code", align_bytes=ALIGN)
+        plan_scale = keep.tile([P, VAR_PASSES, PLANS], U8, name="plan_scale", align_bytes=ALIGN)
+
+        x_group, x_code, x_scale = {}, {}, {}
         s_plane, s_group, s_code, s_scale = {}, {}, {}, {}
-        acc1, acc2, pt = {}, {}, {}
-        copy_v, copy_s = nc.vector.tensor_copy, nc.scalar.copy
+        x_bank, plan_bank, first_bank, second_bank = {}, {}, {}, {}
+
 
         def load_duals(z, u0, u1):
             nc.sync.dma_start(
                 out=x_raw[z][:, u0:u1, :], in_=duals[z].rearrange("(u p) m -> p u m", p=P)[:, u0:u1, :]
             )
 
-        def load_tech(z, h0, h1):
-            b = slice(h0 * 2 * HALF, h1 * 2 * HALF)
+        def load_tech_words(z, h0, h1):
+            b = slice(h0 * 2 * PASS, h1 * 2 * PASS)
             nc.sync.dma_start(
-                out=t_raw[z][:, :, b].bitcast(I32),
-                in_=tech_words[KG * z : KG * (z + 1), :, b].rearrange("g p b -> p g b").bitcast(I32),
+                out=w_raw[z][:, :, b].bitcast(I32),
+                in_=tech_words[ROW_PASSES * z : ROW_PASSES * (z + 1), :, b].rearrange("g p b -> p g b").bitcast(I32),
             )
 
-        def load_scales(q, g0, g1):
-            nc.sync.dma_start(
-                out=ts_raw[32 * q : 32 * q + 4, g0:g1, :].bitcast(I32),
-                in_=tech_scales[g0:g1, 4 * q : 4 * q + 4, :].rearrange("g r n -> r g n").bitcast(I32),
-            )
-
-        def load_cost(h):
-            nc.sync.dma_start(
-                out=rows[NT * h : NT * (h + 1), :].rearrange("t (a q) -> t a q", q=8),
-                in_=cost[h * HALF : (h + 1) * HALF].rearrange("(a t q) -> t a q", t=NT, q=8),
-            )
-
-        def load_intercept():
-            nc.sync.dma_start(
-                out=rows[NT * NH : NT * NH + G * VT, :], in_=intercept.rearrange("z (u p) -> (z u) p", p=P)
-            )
-
-        def load_plans():
-            nc.sync.dma_start(out=plan_b[:], in_=plans_bytes.rearrange("(c p) n -> p c n", p=P))
-
-        def load_plan_scale():
-            nc.sync.dma_start(out=plan_s[:], in_=plans_scale.rearrange("o n -> (o n)").partition_broadcast(P))
-
-        def load_estimate():
-            nc.sync.dma_start(out=est[:], in_=estimate.partition_broadcast(P))
-
-        def split_words(engine_copy, z, u0, u1):
-            if z not in x_word:
-                x_word[z] = work.tile([P, VT, M], BF16, name="x_word", align_bytes=256)
-            engine_copy(
-                out=x_word[z][:, u0:u1, :].bitcast(F32).rearrange("p u (g e w) -> p (u g) e w", g=KG, e=2),
-                in_=x_raw[z][:, u0:u1, :].bitcast(F32).rearrange("p u (g w e) -> p (u g) e w", g=KG, e=2),
-            )
-
-        def TR(z, u):
-            xt[z, u] = bank([P, KG, 2, P], F32)
-            words = (x_word[z] if z in x_word else x_raw[z])[:, u, :].bitcast(F32)
-            for g in range(KG):
-                for e in range(2):
-                    w = (
-                        words[:, 256 * g + P * e : 256 * g + P * (e + 1)]
-                        if z in x_word
-                        else words[:, 256 * g + e : 256 * (g + 1) : 2]
-                    )
-                    nc.tensor.transpose(xt[z, u][:, g, e, :], w, ident[:])
-
-        def XC(engine_copy, z, u):
-            if z not in x_group:
-                x_group[z] = work.tile([P, KG, V * 4], BF16, name="x_group", align_bytes=256)
-            dst = x_group[z][:].bitcast(F32).rearrange("p g (v e) -> p g v e", e=2)
-            engine_copy(out=dst[:, :, u * P : (u + 1) * P, :], in_=xt[z, u][:].rearrange("p g e r -> p g r e"))
-
-        def DQ(z, g, v0, v1):
-            if z not in x_code:
-                x_code[z] = work.tile([P, KG, V], U32, name="x_code", align_bytes=256)
-                x_scale[z] = work.tile([P, KG, V], U8, name="x_scale", align_bytes=256)
-            nc.vector.quantize_mx(
-                out=x_code[z][:, g, v0:v1].bitcast(FP8X4),
-                scales=x_scale[z][:, g, v0:v1],
-                in_=x_group[z][:, g, 4 * v0 : 4 * v1],
-            )
-
-        def TP(z, h0, h1):
-            w = slice(h0 * HALF // 2, h1 * HALF // 2)
-            dst = t_words[z][:].bitcast(I32)[:, :, w]
-            src = t_raw[z][:].bitcast(I32)[:, :, w]
-            if h1 - h0 == NH:
-                dst = dst.rearrange("p g (h t a w) -> p (g h) t a w", h=NH, t=NT, w=4)
-                src = src.rearrange("p g (h a t w) -> p (g h) t a w", h=NH, t=NT, w=4)
-            else:
-                dst = dst.rearrange("p g (t a w) -> p g t a w", t=NT, w=4)
-                src = src.rearrange("p g (a t w) -> p g t a w", t=NT, w=4)
-            nc.vector.tensor_copy(out=dst, in_=src)
-
-        def SP(g0, g1):
-            nc.vector.tensor_copy(
-                out=ts[:, g0:g1, :].bitcast(I32).rearrange("p g (h t a w) -> p (g h) t a w", h=NH, t=NT, w=2),
-                in_=ts_raw[:, g0:g1, :].bitcast(I32).rearrange("p g (h a t w) -> p (g h) t a w", h=NH, t=NT, w=2),
-            )
-
-        def S1(z, h, t):
-            acc1[z, h, t] = bank([P, V], F32)
-            c0 = h * HALF + t * P
-            for g in range(KG):
-                nc.tensor.matmul_mx(
-                    out=acc1[z, h, t][:],
-                    lhsT=t_words[z][:, g, 2 * c0 : 2 * (c0 + P)].bitcast(FP4X4),
-                    lhsT_scale=ts[:, KG * z + g, c0 : c0 + P],
-                    rhs=x_code[z][:, g, :].bitcast(FP8X4),
-                    rhs_scale=x_scale[z][:, g, :],
-                    start=(g == 0),
-                    stop=(g == KG - 1),
+        def load_tech_scales(z0, z1):
+            g = slice(ROW_PASSES * z0, ROW_PASSES * z1)
+            for k in range(4):
+                nc.sync.dma_start(
+                    out=w_scale_raw[32 * k : 32 * k + 4, g, :].bitcast(I32),
+                    in_=tech_scales[g, 4 * k : 4 * k + 4, :].rearrange("g r n -> r g n").bitcast(I32),
                 )
 
-        def EV(z, h, t):
-            if (z, h) not in s_plane:
-                s_plane[z, h] = work.tile([P, NT, V], BF16, name="s_plane", align_bytes=256, bufs=4)
-            j = NT * h + t
-            nc.scalar.activation(
-                out=s_plane[z, h][:, t, :], in_=acc1[z, h, t][:], func=IDENTITY, bias=cols[:, j : j + 1], scale=-1.0
+        def load_variable_rows(rows, row0, vector):
+            for h in range(VAR_PASSES):
+                nc.sync.dma_start(
+                    out=rows[row0 + T * h : row0 + T * (h + 1), :].rearrange("t (a q) -> t a q", q=RUN),
+                    in_=vector[h * PASS : (h + 1) * PASS].rearrange("(a t q) -> t a q", t=T, q=RUN),
+                )
+
+
+        def transpose_duals(z, u):
+            if z not in x_group:
+                x_group[z] = work.tile([P, ROW_PASSES, CUTS * T], BF16, name="x_group", align_bytes=ALIGN)
+            x_bank[z, u] = bank([P, ROW_PASSES, 2, P], F32)
+            words = x_raw[z][:, u, :].bitcast(F32)
+            for g in range(ROW_PASSES):
+                for e in range(2):
+                    nc.tensor.transpose(
+                        x_bank[z, u][:, g, e, :], words[:, PASS // 2 * g + e : PASS // 2 * (g + 1) : 2], ident[:]
+                    )
+            grouped = x_group[z][:].bitcast(F32).rearrange("p g (v e) -> p g v e", e=2)
+            nc.scalar.copy(
+                out=grouped[:, :, u * P : (u + 1) * P, :], in_=x_bank[z, u][:].rearrange("p g e r -> p g r e")
             )
 
-        def GR(engine_copy, z, h, v0, v1):
-            if (z, h) not in s_group:
-                s_group[z, h] = work.tile([P, V, NT], BF16, name="s_group", align_bytes=256, bufs=4)
+        def transpose_dual_pair(z, pair):
+            transpose_duals(z, 2 * pair)
+            transpose_duals(z, 2 * pair + 1)
+
+        def quantize_duals(z, v0, v1):
+            if z not in x_code:
+                x_code[z] = work.tile([P, ROW_PASSES, CUTS], U32, name="x_code", align_bytes=ALIGN)
+                x_scale[z] = work.tile([P, ROW_PASSES, CUTS], U8, name="x_scale", align_bytes=ALIGN)
+            for g in range(ROW_PASSES):
+                nc.vector.quantize_mx(
+                    out=x_code[z][:, g, v0:v1].bitcast(FP8X4),
+                    scales=x_scale[z][:, g, v0:v1],
+                    in_=x_group[z][:, g, T * v0 : T * v1],
+                )
+
+        def quantize_dual_pair(z, pair):
+            quantize_duals(z, 2 * pair * P, 2 * (pair + 1) * P)
+
+
+        def order_tech_half(z, h):
+            words = slice(h * PASS // 2, (h + 1) * PASS // 2)
+            nc.vector.tensor_copy(
+                out=w_code[z][:].bitcast(I32)[:, :, words].rearrange("p g (t a w) -> p g t a w", t=T, w=4),
+                in_=w_raw[z][:].bitcast(I32)[:, :, words].rearrange("p g (a t w) -> p g t a w", t=T, w=4),
+            )
+
+        def order_tech(z):
+            nc.vector.tensor_copy(
+                out=w_code[z][:].bitcast(I32).rearrange("p g (h t a w) -> p (g h) t a w", h=VAR_PASSES, t=T, w=4),
+                in_=w_raw[z][:].bitcast(I32).rearrange("p g (h a t w) -> p (g h) t a w", h=VAR_PASSES, t=T, w=4),
+            )
+
+        def order_tech_scales(z0, z1):
+            g = slice(ROW_PASSES * z0, ROW_PASSES * z1)
+            nc.vector.tensor_copy(
+                out=w_scale[:, g, :].bitcast(I32).rearrange("p g (h t a w) -> p (g h) t a w", h=VAR_PASSES, t=T, w=2),
+                in_=w_scale_raw[:, g, :].bitcast(I32).rearrange("p g (h a t w) -> p (g h) t a w", h=VAR_PASSES, t=T, w=2),
+            )
+
+
+        def first_product(z, h):
+            s_plane[z, h] = work.tile([P, T, CUTS], BF16, name="s_plane", align_bytes=ALIGN, bufs=4)
+            for t in range(T):
+                first_bank[z, h, t] = bank([P, CUTS], F32)
+                n0 = h * PASS + t * P
+                for g in range(ROW_PASSES):
+                    nc.tensor.matmul_mx(
+                        out=first_bank[z, h, t][:],
+                        lhsT=w_code[z][:, g, 2 * n0 : 2 * (n0 + P)].bitcast(FP4X4),
+                        lhsT_scale=w_scale[:, ROW_PASSES * z + g, n0 : n0 + P],
+                        rhs=x_code[z][:, g, :].bitcast(FP8X4),
+                        rhs_scale=x_scale[z][:, g, :],
+                        start=(g == 0),
+                        stop=(g == ROW_PASSES - 1),
+                    )
+                j = COST_COL + T * h + t
+                nc.scalar.activation(
+                    out=s_plane[z, h][:, t, :],
+                    in_=first_bank[z, h, t][:],
+                    func=IDENTITY,
+                    bias=const_cols[:, j : j + 1],
+                    scale=-1.0,
+                )
+
+        def interleave(engine_copy, z, h, v0, v1):
             engine_copy(
                 out=s_group[z, h][:, v0:v1, :].rearrange("p (c i) t -> p c t i", i=4),
                 in_=s_plane[z, h][:, :, v0:v1].rearrange("p t (c i) -> p c t i", i=4),
             )
 
-        def SQ(z, h, v0, v1):
+        def new_slope_group(z, h):
+            s_group[z, h] = work.tile([P, CUTS, T], BF16, name="s_group", align_bytes=ALIGN, bufs=4)
+
+        def group_slopes(z, h):
+            new_slope_group(z, h)
+            interleave(copy_v, z, h, 0, CUTS - SCALAR_CUTS[h])
+            interleave(copy_s, z, h, CUTS - SCALAR_CUTS[h], CUTS)
+
+        def quantize_slopes(z, h, v0=0, v1=CUTS):
             if (z, h) not in s_code:
-                s_code[z, h] = work.tile([P, V], U32, name="s_code", align_bytes=256, bufs=6)
-                s_scale[z, h] = work.tile([P, V], U8, name="s_scale", align_bytes=256, bufs=6)
+                s_code[z, h] = work.tile([P, CUTS], U32, name="s_code", align_bytes=ALIGN, bufs=6)
+                s_scale[z, h] = work.tile([P, CUTS], U8, name="s_scale", align_bytes=ALIGN, bufs=6)
             nc.vector.quantize_mx(
                 out=s_code[z, h][:, v0:v1].bitcast(FP8X4),
                 scales=s_scale[z, h][:, v0:v1],
                 in_=s_group[z, h][:, v0:v1, :].rearrange("p v t -> p (v t)"),
             )
 
-        def S2(z, u, h):
+
+        def second_pass(z, u, h):
             if h == 0:
-                acc2[z, u] = bank([P, C], F32)
-            v = slice(u * P, (u + 1) * P)
+                second_bank[z, u] = bank([P, PLANS], F32)
+            cuts = slice(u * P, (u + 1) * P)
             nc.tensor.matmul_mx(
-                out=acc2[z, u][:],
-                lhsT=s_code[z, h][:, v].bitcast(FP8X4),
-                lhsT_scale=s_scale[z, h][:, v],
-                rhs=plan_c[h][:].bitcast(FP8X4),
-                rhs_scale=plan_sc[h][:],
+                out=second_bank[z, u][:],
+                lhsT=s_code[z, h][:, cuts].bitcast(FP8X4),
+                lhsT_scale=s_scale[z, h][:, cuts],
+                rhs=plan_code[:, h, :].bitcast(FP8X4),
+                rhs_scale=plan_scale[:, h, :],
                 start=(h == 0),
-                stop=(h == NH - 1),
+                stop=(h == VAR_PASSES - 1),
             )
 
-        def FIN(z, u, pieces=1):
-            j = NT * NH + VT * z + u
-            o = outs.tile([P, C], F32, name="o", align_bytes=256)
-            w = C // pieces
-            for c in range(0, C, w):
+        def second_product(z, u):
+            for h in range(VAR_PASSES):
+                second_pass(z, u, h)
+
+        def finish(z, u, pieces=1):
+            j = INTERCEPT_COL + CUT_TILES * z + u
+            o = outs.tile([P, PLANS], F32, name="o", align_bytes=ALIGN)
+            width = PLANS // pieces
+            for c0 in range(0, PLANS, width):
+                c = slice(c0, c0 + width)
                 nc.vector.scalar_tensor_tensor(
-                    out=o[:, c : c + w],
-                    in0=acc2[z, u][:, c : c + w],
-                    scalar=cols[:, j : j + 1],
-                    in1=est[:, z, c : c + w],
+                    out=o[:, c],
+                    in0=second_bank[z, u][:, c],
+                    scalar=const_cols[:, j : j + 1],
+                    in1=est[:, z, c],
                     op0=ADD,
                     op1=SUB,
                 )
-                nc.sync.dma_start(out=out[z, u * P : (u + 1) * P, c : c + w], in_=o[:, c : c + w])
+                nc.sync.dma_start(out=out[z, u * P : (u + 1) * P, c], in_=o[:, c])
 
-        def PM(c):
-            nc.vector.tensor_tensor(
-                out=plan_w[:, c, :], in0=plan_b[:, c, :].bitcast(FP8), in1=plan_s[:], op=MULT
+
+        def widen_plans(c0, c1):
+            nc.vector.tensor_copy(out=plan_wide[:, c0:c1, :], in_=plan_bytes[:, c0:c1, :].bitcast(FP8))
+
+        def order_plans(c0, c1):
+            nc.vector.tensor_copy(
+                out=plan_order[:, c0:c1, :].rearrange("p c (h t a q) -> p (c h) t a q", h=VAR_PASSES, t=T, q=RUN),
+                in_=plan_wide[:, c0:c1, :].rearrange("p c (h a t q) -> p (c h) t a q", h=VAR_PASSES, t=T, q=RUN),
             )
 
-        def PP(engine_copy, c0, c1):
-            engine_copy(
-                out=plan_o[:, c0:c1, :].rearrange("p c (h t a q) -> p (c h) t a q", h=NH, t=NT, q=8),
-                in_=plan_w[:, c0:c1, :].rearrange("p c (h a t q) -> p (c h) t a q", h=NH, t=NT, q=8),
-            )
-
-        def PT(c):
-            pt[c] = bank([P, NH, NT, P], BF16)
-            for h in range(NH):
-                for t in range(NT):
-                    n0 = h * HALF + t * P
-                    nc.tensor.transpose(pt[c][:, h, t, :], plan_o[:, c, n0 : n0 + P], ident_bf[:])
-
-        def PX(c):
-            nc.scalar.copy(out=plan_g[:, :, c * P : (c + 1) * P, :], in_=pt[c][:].rearrange("p h t c -> p h c t"))
-
-        def PQ(h):
-            nc.vector.quantize_mx(
-                out=plan_c[h][:].bitcast(FP8X4),
-                scales=plan_sc[h][:],
-                in_=plan_g[:, h, :, :].rearrange("p c t -> p (c t)"),
-            )
-
-        def CTR():
-            acc2["cols"] = bank([P, P], BF16)
-            nc.tensor.transpose(acc2["cols"][:], rows[:], ident_bf[:])
-            nc.vector.tensor_copy(out=cols[:], in_=acc2["cols"][:, 0:24])
-
-        def load_plan_scale_rows(h):
-            nc.sync.dma_start(
-                out=srow[NT * h : NT * (h + 1), :].rearrange("t (a q) -> t a q", q=8),
-                in_=plans_scale[0, h * HALF : (h + 1) * HALF].rearrange("(a t q) -> t a q", t=NT, q=8),
-            )
-
-        def CTS():
-            acc2["scale"] = bank([P, P], F32)
-            nc.tensor.transpose(acc2["scale"][:], srow[:], ident[:])
-            nc.vector.tensor_copy(out=scol[:], in_=acc2["scale"][:, 0:8])
-
-        def CAST(engine_copy, c0, c1):
-            engine_copy(out=plan_w[:, c0:c1, :], in_=plan_b[:, c0:c1, :].bitcast(FP8))
-
-        def PT2(i, h):
-            pt[i, h] = bank([P, 2, NT, P], BF16)
+        def scale_plans(pair, h):
+            plan_bank[pair, h] = bank([P, 2, T, P], BF16)
             for b in range(2):
-                for t in range(NT):
-                    n0 = h * HALF + t * P
-                    nc.tensor.transpose(pt[i, h][:, b, t, :], plan_o[:, 2 * i + b, n0 : n0 + P], ident_bf[:])
-
-        def PV2(i, h):
+                for t in range(T):
+                    n0 = h * PASS + t * P
+                    nc.tensor.transpose(
+                        plan_bank[pair, h][:, b, t, :], plan_order[:, 2 * pair + b, n0 : n0 + P], ident_bf[:]
+                    )
+            scale = scale_cols[:, T * h : T * (h + 1)]
             nc.vector.tensor_tensor(
-                out=plan_g[:, h, 2 * i * P : 2 * (i + 1) * P, :].rearrange("p (b c) t -> p b c t", b=2),
-                in0=pt[i, h][:].rearrange("p b t c -> p b c t"),
-                in1=scol[:, NT * h : NT * (h + 1)].unsqueeze(1).unsqueeze(1).to_broadcast([P, 2, P, NT]),
+                out=plan_group[:, h, 2 * pair * P : 2 * (pair + 1) * P, :].rearrange("p (b c) t -> p b c t", b=2),
+                in0=plan_bank[pair, h][:].rearrange("p b t c -> p b c t"),
+                in1=scale.unsqueeze(1).unsqueeze(1).to_broadcast([P, 2, P, T]),
                 op=MULT,
             )
 
-        def D():
-            junk = bank([P, V], F32)
-            nc.tensor.matmul(out=junk[:], lhsT=zeros[:, 0:P], rhs=zeros[:], start=True, stop=True)
+        def quantize_plans():
+            for h in range(VAR_PASSES):
+                nc.vector.quantize_mx(
+                    out=plan_code[:, h, :].bitcast(FP8X4),
+                    scales=plan_scale[:, h, :],
+                    in_=plan_group[:, h, :, :].rearrange("p c t -> p (c t)"),
+                )
 
-        zeros = keep.tile([P, V], BF16, name="zeros", align_bytes=256)
-        srow = keep.tile([P, P], F32, name="srow", align_bytes=256)
-        scol = keep.tile([P, 8], F32, name="scol")
+        def constants_to_columns():
+            const_bank = bank([P, P], BF16)
+            nc.tensor.transpose(const_bank[:], const_rows[:], ident_bf[:])
+            nc.vector.tensor_copy(out=const_cols[:], in_=const_bank[:, 0:CONST_COLS])
+            scale_bank = bank([P, P], F32)
+            nc.tensor.transpose(scale_bank[:], scale_rows[:], ident[:])
+            nc.vector.tensor_copy(out=scale_cols[:], in_=scale_bank[:, 0 : VAR_PASSES * T])
+
+        def warm_up(count):
+            for turn in range(count):
+                spare = bank([P, CUTS], F32)
+                nc.tensor.matmul(out=spare[:], lhsT=zeros[:, 0:P], rhs=zeros[:], start=True, stop=True)
+
+
         make_identity(nc, ident[:])
-        nc.vector.memset(ts_raw[:, 0:KG, :].bitcast(I32), 0)
         nc.vector.memset(zeros[:], 0.0)
-        nc.vector.memset(rows[:], 0.0)
-        nc.vector.memset(srow[:], 0.0)
-        nc.vector.memset(warm[:], 0.0)
-        nc.gpsimd.memset(ts_raw[:, KG:, :].bitcast(I32), 0)
+        nc.vector.memset(w_scale_raw[:, 0:ROW_PASSES, :].bitcast(I32), 0)
+        nc.vector.memset(const_rows[:], 0.0)
+        nc.vector.memset(scale_rows[:], 0.0)
+        nc.vector.memset(first_act[:], 0.0)
+        nc.gpsimd.memset(w_scale_raw[:, ROW_PASSES:, :].bitcast(I32), 0)
         nc.vector.tensor_copy(out=ident_bf[:], in_=ident[:])
-        nc.scalar.activation(out=warm[:, 4:8], in_=warm[:, 0:4], func=IDENTITY, bias=0.0, scale=1.0)
+        nc.scalar.activation(out=first_act[:, 4:8], in_=first_act[:, 0:4], func=IDENTITY, bias=0.0, scale=1.0)
 
         load_duals(0, 0, 1)
         load_duals(0, 1, 2)
-        load_scales(0, 0, KG)
-        load_scales(1, 0, KG)
-        load_scales(2, 0, KG)
-        load_scales(3, 0, KG)
         load_duals(0, 2, 4)
-        load_tech(0, 0, 1)
-        load_cost(0)
-        load_cost(1)
-        load_intercept()
+        load_tech_scales(0, 1)
+        load_tech_words(0, 0, 1)
         load_duals(1, 0, 2)
-        load_plan_scale_rows(0)
-        load_plan_scale_rows(1)
-        load_tech(0, 1, 2)
-        load_plans()
+        load_variable_rows(const_rows, COST_COL, cost)
+        nc.sync.dma_start(
+            out=const_rows[INTERCEPT_COL:CONST_COLS, :], in_=intercept.rearrange("z (u p) -> (z u) p", p=P)
+        )
+        load_variable_rows(scale_rows, 0, plans_scale.rearrange("o n -> (o n)"))
+        load_tech_words(0, 1, 2)
+        nc.sync.dma_start(out=plan_bytes[:], in_=plans_bytes.rearrange("(c p) n -> p c n", p=P))
         load_duals(1, 2, 4)
-        load_tech(1, 0, 2)
-        load_scales(0, KG, G * KG)
-        load_scales(1, KG, G * KG)
-        load_scales(2, KG, G * KG)
-        load_scales(3, KG, G * KG)
-        load_duals(2, 0, 4)
-        load_tech(2, 0, 2)
-        load_duals(3, 0, 4)
-        load_tech(3, 0, 2)
-        load_estimate()
-        D()
-        D()
-        D()
-        D()
-        D()
-        D()
-        TR(0, 0)
-        XC(copy_s, 0, 0)
-        TR(0, 1)
-        XC(copy_s, 0, 1)
-        DQ(0, 0, 0, 256)
-        DQ(0, 1, 0, 256)
-        TP(0, 0, 1)
-        D()
-        D()
-        TR(0, 2)
-        XC(copy_s, 0, 2)
-        TR(0, 3)
-        XC(copy_s, 0, 3)
-        CTR()
-        CTS()
-        DQ(0, 0, 256, 512)
-        DQ(0, 1, 256, 512)
-        SP(0, KG)
-        TP(0, 1, 2)
-        D()
-        D()
-        TR(1, 0)
-        XC(copy_s, 1, 0)
-        TR(1, 1)
-        XC(copy_s, 1, 1)
-        S1(0, 0, 0)
-        EV(0, 0, 0)
-        S1(0, 0, 1)
-        EV(0, 0, 1)
-        S1(0, 0, 2)
-        EV(0, 0, 2)
-        S1(0, 0, 3)
-        EV(0, 0, 3)
-        CAST(copy_v, 0, 2)
-        CAST(copy_v, 2, 4)
-        PP(copy_v, 0, 2)
-        TR(1, 2)
-        XC(copy_s, 1, 2)
-        TR(1, 3)
-        XC(copy_s, 1, 3)
-        TP(1, 0, 2)
-        SP(KG, G * KG)
-        S1(0, 1, 0)
-        EV(0, 1, 0)
-        S1(0, 1, 1)
-        EV(0, 1, 1)
-        S1(0, 1, 2)
-        EV(0, 1, 2)
-        S1(0, 1, 3)
-        EV(0, 1, 3)
-        DQ(1, 0, 0, 512)
-        DQ(1, 1, 0, 512)
-        PP(copy_v, 2, 4)
-        GR(copy_v, 0, 0, 0, 320)
-        GR(copy_s, 0, 0, 320, 512)
-        PT2(0, 0)
-        PV2(0, 0)
-        PT2(0, 1)
-        PV2(0, 1)
-        S1(1, 0, 0)
-        EV(1, 0, 0)
-        S1(1, 0, 1)
-        EV(1, 0, 1)
-        S1(1, 0, 2)
-        EV(1, 0, 2)
-        S1(1, 0, 3)
-        EV(1, 0, 3)
-        GR(copy_v, 0, 1, 0, 256)
-        GR(copy_s, 0, 1, 256, 512)
-        PT2(1, 0)
-        PV2(1, 0)
-        PT2(1, 1)
-        PV2(1, 1)
-        SQ(0, 0, 0, 512)
-        S1(1, 1, 0)
-        EV(1, 1, 0)
-        S1(1, 1, 1)
-        EV(1, 1, 1)
-        S1(1, 1, 2)
-        EV(1, 1, 2)
-        S1(1, 1, 3)
-        EV(1, 1, 3)
-        PQ(0)
-        PQ(1)
-        SQ(0, 1, 0, 512)
-        TR(2, 0)
-        XC(copy_s, 2, 0)
-        TR(2, 1)
-        XC(copy_s, 2, 1)
-        GR(copy_s, 1, 0, 256, 512)
-        TP(2, 0, 2)
-        DQ(2, 0, 0, 256)
-        DQ(2, 1, 0, 256)
-        GR(copy_v, 1, 0, 0, 256)
-        S2(0, 0, 0)
-        S2(0, 0, 1)
-        S2(0, 1, 0)
-        S2(0, 1, 1)
-        TR(2, 2)
-        XC(copy_s, 2, 2)
-        TR(2, 3)
-        XC(copy_s, 2, 3)
-        GR(copy_s, 1, 1, 192, 512)
-        GR(copy_v, 1, 1, 0, 192)
-        DQ(2, 0, 256, 512)
-        DQ(2, 1, 256, 512)
-        SQ(1, 0, 0, 512)
-        S2(0, 2, 0)
-        S2(0, 2, 1)
-        S2(0, 3, 0)
-        S2(0, 3, 1)
-        FIN(0, 0)
-        FIN(0, 1)
-        FIN(0, 2)
-        S1(2, 0, 0)
-        EV(2, 0, 0)
-        S1(2, 0, 1)
-        EV(2, 0, 1)
-        S1(2, 0, 2)
-        EV(2, 0, 2)
-        S1(2, 0, 3)
-        EV(2, 0, 3)
-        FIN(0, 3)
-        SQ(1, 1, 0, 512)
-        TP(3, 0, 2)
-        TR(3, 0)
-        XC(copy_s, 3, 0)
-        TR(3, 1)
-        XC(copy_s, 3, 1)
-        GR(copy_s, 2, 0, 320, 512)
-        GR(copy_v, 2, 0, 0, 320)
-        S1(2, 1, 0)
-        EV(2, 1, 0)
-        S1(2, 1, 1)
-        EV(2, 1, 1)
-        S1(2, 1, 2)
-        EV(2, 1, 2)
-        S1(2, 1, 3)
-        EV(2, 1, 3)
-        TR(3, 2)
-        XC(copy_s, 3, 2)
-        TR(3, 3)
-        XC(copy_s, 3, 3)
-        SQ(2, 0, 0, 512)
-        GR(copy_v, 2, 1, 0, 192)
-        DQ(3, 0, 0, 512)
-        DQ(3, 1, 0, 512)
-        GR(copy_s, 2, 1, 192, 512)
-        S2(1, 0, 0)
-        S2(1, 0, 1)
-        S2(1, 1, 0)
-        S2(1, 1, 1)
-        S2(1, 2, 0)
-        S2(1, 2, 1)
-        S2(1, 3, 0)
-        S2(1, 3, 1)
-        FIN(1, 0)
-        FIN(1, 1)
-        SQ(2, 1, 0, 512)
-        FIN(1, 2)
-        FIN(1, 3)
-        S1(3, 0, 0)
-        EV(3, 0, 0)
-        S1(3, 0, 1)
-        EV(3, 0, 1)
-        S1(3, 0, 2)
-        EV(3, 0, 2)
-        S1(3, 0, 3)
-        EV(3, 0, 3)
-        GR(copy_v, 3, 0, 0, 320)
-        GR(copy_s, 3, 0, 320, 512)
-        S2(2, 0, 0)
-        S2(2, 0, 1)
-        S2(2, 1, 0)
-        S2(2, 1, 1)
-        FIN(2, 0)
-        FIN(2, 1)
-        S1(3, 1, 0)
-        EV(3, 1, 0)
-        S1(3, 1, 1)
-        EV(3, 1, 1)
-        S1(3, 1, 2)
-        EV(3, 1, 2)
-        S1(3, 1, 3)
-        EV(3, 1, 3)
-        SQ(3, 0, 0, 512)
-        S2(2, 2, 0)
-        S2(2, 2, 1)
-        S2(2, 3, 0)
-        S2(2, 3, 1)
-        S2(3, 0, 0)
-        S2(3, 1, 0)
-        S2(3, 2, 0)
-        S2(3, 3, 0)
-        FIN(2, 2)
-        GR(copy_v, 3, 1, 0, 256)
-        GR(copy_s, 3, 1, 256, 448)
-        GR(copy_v, 3, 1, 448, 512)
-        SQ(3, 1, 0, 256)
-        SQ(3, 1, 256, 512)
-        FIN(2, 3)
-        S2(3, 0, 1)
-        FIN(3, 0)
-        S2(3, 1, 1)
-        FIN(3, 1)
-        S2(3, 2, 1)
-        FIN(3, 2)
-        S2(3, 3, 1)
-        FIN(3, 3, 2)
+        load_tech_words(1, 0, 2)
+        load_tech_scales(1, SCENARIOS)
+        for z in (2, 3):
+            load_duals(z, 0, 4)
+            load_tech_words(z, 0, 2)
+        nc.sync.dma_start(out=est[:], in_=estimate.partition_broadcast(P))
+
+        warm_up(4)
+        transpose_dual_pair(0, 0)
+        quantize_dual_pair(0, 0)
+        order_tech_half(0, 0)
+        warm_up(2)
+        transpose_dual_pair(0, 1)
+        constants_to_columns()
+        quantize_dual_pair(0, 1)
+        order_tech_scales(0, 1)
+        order_tech_half(0, 1)
+        warm_up(2)
+        transpose_dual_pair(1, 0)
+
+        first_product(0, 0)
+        widen_plans(0, 2)
+        widen_plans(2, 4)
+        order_plans(0, 2)
+        transpose_dual_pair(1, 1)
+        order_tech(1)
+        order_tech_scales(1, SCENARIOS)
+        first_product(0, 1)
+        quantize_duals(1, 0, CUTS)
+        order_plans(2, 4)
+        group_slopes(0, 0)
+        for h in range(VAR_PASSES):
+            scale_plans(0, h)
+
+        first_product(1, 0)
+        group_slopes(0, 1)
+        for h in range(VAR_PASSES):
+            scale_plans(1, h)
+        quantize_slopes(0, 0)
+        first_product(1, 1)
+        quantize_plans()
+        quantize_slopes(0, 1)
+
+        transpose_dual_pair(2, 0)
+        order_tech(2)
+        quantize_dual_pair(2, 0)
+        group_slopes(1, 0)
+        second_product(0, 0)
+        second_product(0, 1)
+        transpose_dual_pair(2, 1)
+        group_slopes(1, 1)
+        quantize_dual_pair(2, 1)
+        quantize_slopes(1, 0)
+        second_product(0, 2)
+        second_product(0, 3)
+        for u in range(3):
+            finish(0, u)
+
+        first_product(2, 0)
+        finish(0, 3)
+        quantize_slopes(1, 1)
+        order_tech(3)
+        transpose_dual_pair(3, 0)
+        group_slopes(2, 0)
+        first_product(2, 1)
+        transpose_dual_pair(3, 1)
+        quantize_slopes(2, 0)
+        group_slopes(2, 1)
+        quantize_duals(3, 0, CUTS)
+        for u in range(CUT_TILES):
+            second_product(1, u)
+        finish(1, 0)
+        finish(1, 1)
+        quantize_slopes(2, 1)
+        finish(1, 2)
+        finish(1, 3)
+
+        first_product(3, 0)
+        group_slopes(3, 0)
+        second_product(2, 0)
+        second_product(2, 1)
+        finish(2, 0)
+        finish(2, 1)
+        first_product(3, 1)
+        quantize_slopes(3, 0)
+        second_product(2, 2)
+        second_product(2, 3)
+        for u in range(CUT_TILES):
+            second_pass(3, u, 0)
+        finish(2, 2)
+        new_slope_group(3, 1)
+        interleave(copy_v, 3, 1, 0, 256)
+        interleave(copy_s, 3, 1, 256, 448)
+        interleave(copy_v, 3, 1, 448, 512)
+        quantize_slopes(3, 1, 0, 256)
+        quantize_slopes(3, 1, 256, 512)
+        finish(2, 3)
+        for u in range(CUT_TILES):
+            second_pass(3, u, 1)
+            finish(3, u, pieces=2 if u == CUT_TILES - 1 else 1)

from contextlib import ExitStack

import concourse.mybir as mybir
from concourse.masks import make_identity

SCENARIOS, CUTS, ROWS, VARS, PLANS = 4, 512, 1024, 1024, 512
FLOPS = SCENARIOS * (2 * CUTS * ROWS * VARS + 2 * CUTS * VARS * PLANS)

F32 = mybir.dt.float32
BF16 = mybir.dt.bfloat16
I32 = mybir.dt.int32
U32 = mybir.dt.uint32
U8 = mybir.dt.uint8
FP8 = mybir.dt.float8_e4m3fn
FP8X4 = mybir.dt.float8_e4m3fn_x4
FP4X4 = mybir.dt.float4_e2m1fn_x4
ADD = mybir.AluOpType.add
SUB = mybir.AluOpType.subtract
MULT = mybir.AluOpType.mult
IDENTITY = mybir.ActivationFunctionType.Identity

P = 128
T = 4
PASS = P * T
ROW_PASSES = ROWS // PASS
VAR_PASSES = VARS // PASS
RUN = 8
CUT_TILES = CUTS // P
PLAN_TILES = PLANS // P
COST_COL, INTERCEPT_COL = 0, VAR_PASSES * T
CONST_COLS = INTERCEPT_COL + SCENARIOS * CUT_TILES
ALIGN = 256

SCALAR_CUTS = (192, 320)


def tile_benders_cut_evaluation_s14_kernel(
    tc, duals, tech_words, tech_scales, cost, plans_bytes, plans_scale, intercept, estimate, out
):
    nc = tc.nc
    copy_v, copy_s = nc.vector.tensor_copy, nc.scalar.copy

    with ExitStack() as ctx:
        keep = ctx.enter_context(tc.tile_pool(name="keep", bufs=1))
        work = ctx.enter_context(tc.tile_pool(name="work", bufs=2))
        outs = ctx.enter_context(tc.tile_pool(name="outs", bufs=6))
        psum = ctx.enter_context(tc.psum_pool(name="psum", bufs=8))
        ctx.enter_context(tc.manual_schedule())

        def bank(shape, dtype):
            return psum.tile(shape, dtype, name="bank", tag="bank")

        def by_scenario(name, shape, dtype):
            return [keep.tile(shape, dtype, name=f"{name}{z}", align_bytes=ALIGN) for z in range(SCENARIOS)]

        ident = keep.tile([P, P], F32, name="ident")
        ident_bf = keep.tile([P, P], BF16, name="ident_bf")
        zeros = keep.tile([P, CUTS], BF16, name="zeros", align_bytes=ALIGN)
        first_act = keep.tile([P, 8], F32, name="first_act")
        const_rows = keep.tile([P, P], BF16, name="const_rows")
        const_cols = keep.tile([P, CONST_COLS], F32, name="const_cols")
        scale_rows = keep.tile([P, P], F32, name="scale_rows", align_bytes=ALIGN)
        scale_cols = keep.tile([P, VAR_PASSES * T], F32, name="scale_cols")
        est = keep.tile([P, SCENARIOS, PLANS], BF16, name="est", align_bytes=ALIGN)

        x_raw = by_scenario("x_raw", [P, CUT_TILES, ROWS], BF16)
        w_raw = by_scenario("w_raw", [P, ROW_PASSES, 2 * VARS], U8)
        w_code = by_scenario("w_code", [P, ROW_PASSES, 2 * VARS], U8)
        w_scale_raw = keep.tile([P, SCENARIOS * ROW_PASSES, VARS], U8, name="w_scale_raw", align_bytes=ALIGN)
        w_scale = keep.tile([P, SCENARIOS * ROW_PASSES, VARS], U8, name="w_scale", align_bytes=ALIGN)

        plan_bytes = keep.tile([P, PLAN_TILES, VARS], U8, name="plan_bytes", align_bytes=ALIGN)
        plan_wide = keep.tile([P, PLAN_TILES, VARS], BF16, name="plan_wide", align_bytes=ALIGN)
        plan_order = keep.tile([P, PLAN_TILES, VARS], BF16, name="plan_order", align_bytes=ALIGN)
        plan_group = keep.tile([P, VAR_PASSES, PLANS, T], BF16, name="plan_group", align_bytes=ALIGN)
        plan_code = keep.tile([P, VAR_PASSES, PLANS], U32, name="plan_code", align_bytes=ALIGN)
        plan_scale = keep.tile([P, VAR_PASSES, PLANS], U8, name="plan_scale", align_bytes=ALIGN)

        x_group, x_code, x_scale = {}, {}, {}
        s_plane, s_group, s_code, s_scale = {}, {}, {}, {}
        x_bank, plan_bank, first_bank, second_bank = {}, {}, {}, {}


        def load_duals(z, u0, u1):
            nc.sync.dma_start(
                out=x_raw[z][:, u0:u1, :], in_=duals[z].rearrange("(u p) m -> p u m", p=P)[:, u0:u1, :]
            )

        def load_tech_words(z, h0, h1):
            b = slice(h0 * 2 * PASS, h1 * 2 * PASS)
            nc.sync.dma_start(
                out=w_raw[z][:, :, b].bitcast(I32),
                in_=tech_words[ROW_PASSES * z : ROW_PASSES * (z + 1), :, b].rearrange("g p b -> p g b").bitcast(I32),
            )

        def load_tech_scales(z0, z1):
            g = slice(ROW_PASSES * z0, ROW_PASSES * z1)
            for k in range(4):
                nc.sync.dma_start(
                    out=w_scale_raw[32 * k : 32 * k + 4, g, :].bitcast(I32),
                    in_=tech_scales[g, 4 * k : 4 * k + 4, :].rearrange("g r n -> r g n").bitcast(I32),
                )

        def load_variable_rows(rows, row0, vector):
            for h in range(VAR_PASSES):
                nc.sync.dma_start(
                    out=rows[row0 + T * h : row0 + T * (h + 1), :].rearrange("t (a q) -> t a q", q=RUN),
                    in_=vector[h * PASS : (h + 1) * PASS].rearrange("(a t q) -> t a q", t=T, q=RUN),
                )


        def transpose_duals(z, u):
            if z not in x_group:
                x_group[z] = work.tile([P, ROW_PASSES, CUTS * T], BF16, name="x_group", align_bytes=ALIGN)
            x_bank[z, u] = bank([P, ROW_PASSES, 2, P], F32)
            words = x_raw[z][:, u, :].bitcast(F32)
            for g in range(ROW_PASSES):
                for e in range(2):
                    nc.tensor.transpose(
                        x_bank[z, u][:, g, e, :], words[:, PASS // 2 * g + e : PASS // 2 * (g + 1) : 2], ident[:]
                    )
            grouped = x_group[z][:].bitcast(F32).rearrange("p g (v e) -> p g v e", e=2)
            nc.scalar.copy(
                out=grouped[:, :, u * P : (u + 1) * P, :], in_=x_bank[z, u][:].rearrange("p g e r -> p g r e")
            )

        def transpose_dual_pair(z, pair):
            transpose_duals(z, 2 * pair)
            transpose_duals(z, 2 * pair + 1)

        def quantize_duals(z, v0, v1):
            if z not in x_code:
                x_code[z] = work.tile([P, ROW_PASSES, CUTS], U32, name="x_code", align_bytes=ALIGN)
                x_scale[z] = work.tile([P, ROW_PASSES, CUTS], U8, name="x_scale", align_bytes=ALIGN)
            for g in range(ROW_PASSES):
                nc.vector.quantize_mx(
                    out=x_code[z][:, g, v0:v1].bitcast(FP8X4),
                    scales=x_scale[z][:, g, v0:v1],
                    in_=x_group[z][:, g, T * v0 : T * v1],
                )

        def quantize_dual_pair(z, pair):
            quantize_duals(z, 2 * pair * P, 2 * (pair + 1) * P)


        def order_tech_half(z, h):
            words = slice(h * PASS // 2, (h + 1) * PASS // 2)
            nc.vector.tensor_copy(
                out=w_code[z][:].bitcast(I32)[:, :, words].rearrange("p g (t a w) -> p g t a w", t=T, w=4),
                in_=w_raw[z][:].bitcast(I32)[:, :, words].rearrange("p g (a t w) -> p g t a w", t=T, w=4),
            )

        def order_tech(z):
            nc.vector.tensor_copy(
                out=w_code[z][:].bitcast(I32).rearrange("p g (h t a w) -> p (g h) t a w", h=VAR_PASSES, t=T, w=4),
                in_=w_raw[z][:].bitcast(I32).rearrange("p g (h a t w) -> p (g h) t a w", h=VAR_PASSES, t=T, w=4),
            )

        def order_tech_scales(z0, z1):
            g = slice(ROW_PASSES * z0, ROW_PASSES * z1)
            nc.vector.tensor_copy(
                out=w_scale[:, g, :].bitcast(I32).rearrange("p g (h t a w) -> p (g h) t a w", h=VAR_PASSES, t=T, w=2),
                in_=w_scale_raw[:, g, :].bitcast(I32).rearrange("p g (h a t w) -> p (g h) t a w", h=VAR_PASSES, t=T, w=2),
            )


        def first_product(z, h):
            s_plane[z, h] = work.tile([P, T, CUTS], BF16, name="s_plane", align_bytes=ALIGN, bufs=4)
            for t in range(T):
                first_bank[z, h, t] = bank([P, CUTS], F32)
                n0 = h * PASS + t * P
                for g in range(ROW_PASSES):
                    nc.tensor.matmul_mx(
                        out=first_bank[z, h, t][:],
                        lhsT=w_code[z][:, g, 2 * n0 : 2 * (n0 + P)].bitcast(FP4X4),
                        lhsT_scale=w_scale[:, ROW_PASSES * z + g, n0 : n0 + P],
                        rhs=x_code[z][:, g, :].bitcast(FP8X4),
                        rhs_scale=x_scale[z][:, g, :],
                        start=(g == 0),
                        stop=(g == ROW_PASSES - 1),
                    )
                j = COST_COL + T * h + t
                nc.scalar.activation(
                    out=s_plane[z, h][:, t, :],
                    in_=first_bank[z, h, t][:],
                    func=IDENTITY,
                    bias=const_cols[:, j : j + 1],
                    scale=-1.0,
                )

        def interleave(engine_copy, z, h, v0, v1):
            engine_copy(
                out=s_group[z, h][:, v0:v1, :].rearrange("p (c i) t -> p c t i", i=4),
                in_=s_plane[z, h][:, :, v0:v1].rearrange("p t (c i) -> p c t i", i=4),
            )

        def new_slope_group(z, h):
            s_group[z, h] = work.tile([P, CUTS, T], BF16, name="s_group", align_bytes=ALIGN, bufs=4)

        def group_slopes(z, h):
            new_slope_group(z, h)
            interleave(copy_v, z, h, 0, CUTS - SCALAR_CUTS[h])
            interleave(copy_s, z, h, CUTS - SCALAR_CUTS[h], CUTS)

        def quantize_slopes(z, h, v0=0, v1=CUTS):
            if (z, h) not in s_code:
                s_code[z, h] = work.tile([P, CUTS], U32, name="s_code", align_bytes=ALIGN, bufs=6)
                s_scale[z, h] = work.tile([P, CUTS], U8, name="s_scale", align_bytes=ALIGN, bufs=6)
            nc.vector.quantize_mx(
                out=s_code[z, h][:, v0:v1].bitcast(FP8X4),
                scales=s_scale[z, h][:, v0:v1],
                in_=s_group[z, h][:, v0:v1, :].rearrange("p v t -> p (v t)"),
            )


        def second_pass(z, u, h):
            if h == 0:
                second_bank[z, u] = bank([P, PLANS], F32)
            cuts = slice(u * P, (u + 1) * P)
            nc.tensor.matmul_mx(
                out=second_bank[z, u][:],
                lhsT=s_code[z, h][:, cuts].bitcast(FP8X4),
                lhsT_scale=s_scale[z, h][:, cuts],
                rhs=plan_code[:, h, :].bitcast(FP8X4),
                rhs_scale=plan_scale[:, h, :],
                start=(h == 0),
                stop=(h == VAR_PASSES - 1),
            )

        def second_product(z, u):
            for h in range(VAR_PASSES):
                second_pass(z, u, h)

        def finish(z, u, pieces=1):
            j = INTERCEPT_COL + CUT_TILES * z + u
            o = outs.tile([P, PLANS], F32, name="o", align_bytes=ALIGN)
            width = PLANS // pieces
            for c0 in range(0, PLANS, width):
                c = slice(c0, c0 + width)
                nc.vector.scalar_tensor_tensor(
                    out=o[:, c],
                    in0=second_bank[z, u][:, c],
                    scalar=const_cols[:, j : j + 1],
                    in1=est[:, z, c],
                    op0=ADD,
                    op1=SUB,
                )
                nc.sync.dma_start(out=out[z, u * P : (u + 1) * P, c], in_=o[:, c])


        def widen_plans(c0, c1):
            nc.vector.tensor_copy(out=plan_wide[:, c0:c1, :], in_=plan_bytes[:, c0:c1, :].bitcast(FP8))

        def order_plans(c0, c1):
            nc.vector.tensor_copy(
                out=plan_order[:, c0:c1, :].rearrange("p c (h t a q) -> p (c h) t a q", h=VAR_PASSES, t=T, q=RUN),
                in_=plan_wide[:, c0:c1, :].rearrange("p c (h a t q) -> p (c h) t a q", h=VAR_PASSES, t=T, q=RUN),
            )

        def scale_plans(pair, h):
            plan_bank[pair, h] = bank([P, 2, T, P], BF16)
            for b in range(2):
                for t in range(T):
                    n0 = h * PASS + t * P
                    nc.tensor.transpose(
                        plan_bank[pair, h][:, b, t, :], plan_order[:, 2 * pair + b, n0 : n0 + P], ident_bf[:]
                    )
            scale = scale_cols[:, T * h : T * (h + 1)]
            nc.vector.tensor_tensor(
                out=plan_group[:, h, 2 * pair * P : 2 * (pair + 1) * P, :].rearrange("p (b c) t -> p b c t", b=2),
                in0=plan_bank[pair, h][:].rearrange("p b t c -> p b c t"),
                in1=scale.unsqueeze(1).unsqueeze(1).to_broadcast([P, 2, P, T]),
                op=MULT,
            )

        def quantize_plans():
            for h in range(VAR_PASSES):
                nc.vector.quantize_mx(
                    out=plan_code[:, h, :].bitcast(FP8X4),
                    scales=plan_scale[:, h, :],
                    in_=plan_group[:, h, :, :].rearrange("p c t -> p (c t)"),
                )

        def constants_to_columns():
            const_bank = bank([P, P], BF16)
            nc.tensor.transpose(const_bank[:], const_rows[:], ident_bf[:])
            nc.vector.tensor_copy(out=const_cols[:], in_=const_bank[:, 0:CONST_COLS])
            scale_bank = bank([P, P], F32)
            nc.tensor.transpose(scale_bank[:], scale_rows[:], ident[:])
            nc.vector.tensor_copy(out=scale_cols[:], in_=scale_bank[:, 0 : VAR_PASSES * T])

        def warm_up(count):
            for turn in range(count):
                spare = bank([P, CUTS], F32)
                nc.tensor.matmul(out=spare[:], lhsT=zeros[:, 0:P], rhs=zeros[:], start=True, stop=True)


        make_identity(nc, ident[:])
        nc.vector.memset(zeros[:], 0.0)
        nc.vector.memset(w_scale_raw[:, 0:ROW_PASSES, :].bitcast(I32), 0)
        nc.vector.memset(const_rows[:], 0.0)
        nc.vector.memset(scale_rows[:], 0.0)
        nc.vector.memset(first_act[:], 0.0)
        nc.gpsimd.memset(w_scale_raw[:, ROW_PASSES:, :].bitcast(I32), 0)
        nc.vector.tensor_copy(out=ident_bf[:], in_=ident[:])
        nc.scalar.activation(out=first_act[:, 4:8], in_=first_act[:, 0:4], func=IDENTITY, bias=0.0, scale=1.0)

        load_duals(0, 0, 1)
        load_duals(0, 1, 2)
        load_duals(0, 2, 4)
        load_tech_scales(0, 1)
        load_tech_words(0, 0, 1)
        load_duals(1, 0, 2)
        load_variable_rows(const_rows, COST_COL, cost)
        nc.sync.dma_start(
            out=const_rows[INTERCEPT_COL:CONST_COLS, :], in_=intercept.rearrange("z (u p) -> (z u) p", p=P)
        )
        load_variable_rows(scale_rows, 0, plans_scale.rearrange("o n -> (o n)"))
        load_tech_words(0, 1, 2)
        nc.sync.dma_start(out=plan_bytes[:], in_=plans_bytes.rearrange("(c p) n -> p c n", p=P))
        load_duals(1, 2, 4)
        load_tech_words(1, 0, 2)
        load_tech_scales(1, SCENARIOS)
        for z in (2, 3):
            load_duals(z, 0, 4)
            load_tech_words(z, 0, 2)
        nc.sync.dma_start(out=est[:], in_=estimate.partition_broadcast(P))

        warm_up(4)
        transpose_dual_pair(0, 0)
        quantize_dual_pair(0, 0)
        order_tech_half(0, 0)
        warm_up(2)
        transpose_dual_pair(0, 1)
        constants_to_columns()
        quantize_dual_pair(0, 1)
        order_tech_scales(0, 1)
        order_tech_half(0, 1)
        warm_up(2)
        transpose_dual_pair(1, 0)

        first_product(0, 0)
        widen_plans(0, 2)
        widen_plans(2, 4)
        order_plans(0, 2)
        transpose_dual_pair(1, 1)
        order_tech(1)
        order_tech_scales(1, SCENARIOS)
        first_product(0, 1)
        quantize_duals(1, 0, CUTS)
        order_plans(2, 4)
        group_slopes(0, 0)
        for h in range(VAR_PASSES):
            scale_plans(0, h)

        first_product(1, 0)
        group_slopes(0, 1)
        for h in range(VAR_PASSES):
            scale_plans(1, h)
        quantize_slopes(0, 0)
        first_product(1, 1)
        quantize_plans()
        quantize_slopes(0, 1)

        transpose_dual_pair(2, 0)
        order_tech(2)
        quantize_dual_pair(2, 0)
        group_slopes(1, 0)
        second_product(0, 0)
        second_product(0, 1)
        transpose_dual_pair(2, 1)
        group_slopes(1, 1)
        quantize_dual_pair(2, 1)
        quantize_slopes(1, 0)
        second_product(0, 2)
        second_product(0, 3)
        for u in range(3):
            finish(0, u)

        first_product(2, 0)
        finish(0, 3)
        quantize_slopes(1, 1)
        order_tech(3)
        transpose_dual_pair(3, 0)
        group_slopes(2, 0)
        first_product(2, 1)
        transpose_dual_pair(3, 1)
        quantize_slopes(2, 0)
        group_slopes(2, 1)
        quantize_duals(3, 0, CUTS)
        for u in range(CUT_TILES):
            second_product(1, u)
        finish(1, 0)
        finish(1, 1)
        quantize_slopes(2, 1)
        finish(1, 2)
        finish(1, 3)

        first_product(3, 0)
        group_slopes(3, 0)
        second_product(2, 0)
        second_product(2, 1)
        finish(2, 0)
        finish(2, 1)
        first_product(3, 1)
        quantize_slopes(3, 0)
        second_product(2, 2)
        second_product(2, 3)
        for u in range(CUT_TILES):
            second_pass(3, u, 0)
        finish(2, 2)
        new_slope_group(3, 1)
        interleave(copy_v, 3, 1, 0, 256)
        interleave(copy_s, 3, 1, 256, 448)
        interleave(copy_v, 3, 1, 448, 512)
        quantize_slopes(3, 1, 0, 256)
        quantize_slopes(3, 1, 256, 512)
        finish(2, 3)
        for u in range(CUT_TILES):
            second_pass(3, u, 1)
            finish(3, u, pieces=2 if u == CUT_TILES - 1 else 1)
